import numpy as np
import ml_dtypes


def mxq(x, axis, fmt="e4m3"):
    dtype, down = {"e4m3": (ml_dtypes.float8_e4m3fn, 7), "e5m2": (ml_dtypes.float8_e5m2, 14)}[fmt]
    v = np.moveaxis(np.asarray(x, np.float32).astype(ml_dtypes.bfloat16).astype(np.float64), axis, -1)
    blocks = v.reshape(v.shape[:-1] + (-1, 32))
    amax = np.abs(blocks).max(-1, keepdims=True)
    byte = np.maximum(np.where(amax > 0, np.frexp(amax)[1] - 1 + 127, 0) - down, 1)
    scale = np.exp2(byte - 127.0)
    codes = (blocks / scale).astype(np.float32).astype(dtype).astype(np.float64)
    return np.moveaxis((codes * scale).reshape(v.shape), -1, axis)


WIDE = False


def mx_kscale(k):
    if not WIDE:
        return np.ones(k)
    levels = np.array([10, -10, 5, -5, 0])
    if k % 512:
        return np.exp2(np.random.permutation(np.resize(levels, k // 32))).repeat(32)
    a = np.empty((k // 512, 16))
    for p in range(k // 512):
        a[p, :8] = np.random.permutation(np.resize(levels, 8))
        for g in range(8):
            far = levels[np.abs(levels - a[p, g]) >= 10]
            a[p, g + 8] = far[np.random.randint(len(far))]
    return np.exp2(a.ravel()).repeat(32)


def f64(x):
    return np.asarray(x).astype(np.float64)


def striped(idx):
    return np.tile(idx.reshape(-1, 16).T, (8, 1)).astype(np.uint16)


def unstriped(offs):
    return offs[:16].T.reshape(-1).astype(np.int64)


def striped8(idx):
    return np.concatenate([x.reshape(-1, 16).T for x in idx]).astype(np.uint16)


def runs(offs, k):
    lists = np.stack([offs[16 * r : 16 * r + 16].T.reshape(-1) for r in range(8)]).astype(np.int64)
    return lists[np.arange(k) % 512 // 64]


def pack_weight(w):
    k, n = w.shape
    w = f64(np.asarray(w, np.float32).astype(ml_dtypes.bfloat16)).reshape(k // 32, 32, n)
    amax = np.abs(w).max(1)
    byte = np.clip(np.where(amax > 0, np.frexp(amax)[1] - 1 + 127 - 7, 1), 1, 254)
    scaled = (w * np.exp2(127.0 - byte)[:, None, :]).reshape(k, n).astype(np.float32)
    words = np.ascontiguousarray(scaled.reshape(k // 512, 128, 4, n).transpose(0, 1, 3, 2)).astype(ml_dtypes.float8_e4m3fn).view(np.uint8)
    return words, np.ascontiguousarray(byte.astype(np.uint8).reshape(k // 512, 16, n))


def unpack_weight(words, scales):
    g, p, n, _ = words.shape
    vals = np.ascontiguousarray(words).view(ml_dtypes.float8_e4m3fn).astype(np.float64) * np.repeat(np.exp2(scales.astype(np.float64) - 127.0), 8, axis=1)[..., None]
    return vals.transpose(0, 1, 3, 2).reshape(g * 512, n)


def sigmoid(v):
    return 1.0 / (1.0 + np.exp(-np.maximum(v, -700.0)))

def planes(y):
    n, m = y.shape
    v = y.astype(np.float32).astype(ml_dtypes.bfloat16).astype(np.float64).reshape(n // 32, 32, m)
    top = np.abs(v).max(1)
    byte = np.clip(np.where(top > 0, np.frexp(top)[1] - 1 + 127 - 7, 1), 1, 254)
    codes = (v * np.exp2(127.0 - byte)[:, None, :]).reshape(n, m).astype(np.float32).astype(ml_dtypes.float8_e4m3fn).view(np.uint8)
    words = codes.reshape(n // 512, 128, 4, m).transpose(0, 1, 3, 2)
    return np.ascontiguousarray(words), np.ascontiguousarray(byte.astype(np.uint8).reshape(n // 512, 16, m))


K, T, S, N, H = 512, 2048, 512, 512, 512


def setup_inputs():
    n = np.random.standard_normal
    s = mx_kscale(K)[:, None]
    u = mx_kscale(H)
    packed_xT = pack_weight(n((K, T)) * s)
    packed_w1 = pack_weight(n((K, H)) / np.sqrt(K) / s)
    packed_w2 = pack_weight(n((K, H)) / np.sqrt(K) / s)
    packed_w3 = pack_weight(n((K, H)) / np.sqrt(K) / s)
    packed_w4 = pack_weight(n((H, N)) / np.sqrt(H) / u[:, None])
    return {
        "x_words": packed_xT[0],
        "x_scales": packed_xT[1],
        "w1_words": packed_w1[0],
        "w1_scales": packed_w1[1],
        "w2_words": packed_w2[0],
        "w2_scales": packed_w2[1],
        "w3_words": packed_w3[0],
        "w3_scales": packed_w3[1],
        "tau": np.random.uniform(0.3, 0.9, (H, 1)).astype(np.float32),
        "gn": (np.random.uniform(0.5, 1.5, (H, 1)) * u[:, None]).astype(np.float32),
        "w4_words": packed_w4[0],
        "w4_scales": packed_w4[1],
        "sl": np.random.uniform(1.0, 2.0, (N, 1)).astype(np.float32),
        "th": (0.5 * n((N, 1))).astype(np.float32),
        "offs": striped(np.random.permutation(T)[:S]),
        "two": striped(np.random.permutation(T)[:S]),
        "three": striped(np.random.permutation(T)[:S]),
        "n1": striped(np.random.permutation(S)),
        "n2": striped(np.random.permutation(S)),
        "n3": striped(np.random.permutation(S)),
        "n4": striped(np.random.permutation(S)),
        "n5": striped8(np.stack([np.random.permutation(S) for _ in range(8)])),
        "n6": striped8(np.stack([np.random.permutation(S) for _ in range(8)])),
        "n7": striped8(np.stack([np.random.permutation(S) for _ in range(8)])),
    }


def reference(x_words, x_scales, w1_words, w1_scales, w2_words, w2_scales, w3_words, w3_scales, tau, gn, w4_words, w4_scales, sl, th, offs, two, three, n1, n2, n3, n4, n5, n6, n7):
    x_three = unpack_weight(x_words, x_scales)[:, unstriped(three)]
    b = unpack_weight(w3_words, w3_scales).T @ x_three
    top = b.max(axis=1, keepdims=True)
    ea = np.exp(f64(tau) * (b[:, unstriped(n3)] - top))
    xq = unpack_weight(x_words, x_scales)[:, unstriped(offs)]
    y = unpack_weight(w1_words, w1_scales).T @ xq
    x_two = unpack_weight(x_words, x_scales)[:, unstriped(two)]
    d = unpack_weight(w2_words, w2_scales).T @ x_two
    m1 = (y - y[:, unstriped(n1)]) / (np.abs(d) + np.abs(d[:, unstriped(n2)]) + 0.5)
    z = f64(gn) * ((2.0 * ea) * (m1 - m1[:, unstriped(n4)]) - (0.5 * b))
    h = unpack_weight(w4_words, w4_scales).T @ mxq(z, 0, "e4m3")
    own = sigmoid(f64(sl) * (h - f64(th)))
    sg = sigmoid(f64(sl) * (h[np.arange(N)[:, None], runs(n5, N)] - f64(th)))
    out_0 = (h[np.arange(N)[:, None], runs(n6, N)]) * own + (h[np.arange(N)[:, None], runs(n7, N)]) * sg
    return (out_0,) + planes(out_0)

@@ -1,0 +1,238 @@
+from contextlib import ExitStack
+
+import concourse.mybir as mybir
+
+F32 = mybir.dt.float32
+BF16 = mybir.dt.bfloat16
+I32 = mybir.dt.int32
+U32 = mybir.dt.uint32
+U16 = mybir.dt.uint16
+U8 = mybir.dt.uint8
+FP8X4 = mybir.dt.float8_e4m3fn_x4
+ALU = mybir.AluOpType
+ACT = mybir.ActivationFunctionType
+
+P = 128
+PACK = 4
+TOKENS = 2048
+S = 512
+HALF = S // 2
+LIST_COLS = S // 16
+FLOPS = 4 * 2 * 512 * 512 * 512
+
+
+def tile_picked_trionormbpxbemx_none_po_kernel(
+    tc, x_words, x_scales, w1_words, w1_scales, w2_words, w2_scales, w3_words, w3_scales, tau, gn,
+    w4_words, w4_scales, sl, th, offs, two, three, n1, n2, n3, n4, n5, n6, n7, out_0, out_1, out_2,
+):
+    nc = tc.nc
+    tiles = range(PACK)
+    halves = range(2)
+
+    with ExitStack() as ctx:
+        keep = ctx.enter_context(tc.tile_pool(name="keep", bufs=1))
+        psum = ctx.enter_context(tc.psum_pool(name="psum", bufs=1))
+
+        def cols(half):
+            return slice(half * HALF, (half + 1) * HALF)
+
+        def load_list(name, src):
+            tile = keep.tile([P, LIST_COLS], U16, name=name)
+            nc.sync.dma_start(tile[:], src)
+            return tile
+
+        def part(lst, half):
+            return lst[:, half * LIST_COLS // 2 : (half + 1) * LIST_COLS // 2]
+
+        def load_words(name, src, width):
+            tile = keep.tile([P, width], U32, name=name, align_bytes=64)
+            nc.sync.dma_start(tile[:].bitcast(I32), src[0].rearrange("p n t -> p (n t)").bitcast(I32))
+            return tile
+
+        def load_scale_rows(queue, tile, src, row):
+            for r in range(4):
+                every_fourth = src[0, r::4, :].bitcast(I32)
+                queue.dma_start(tile[row + r :: 8, :].bitcast(I32), every_fourth.unsqueeze(1).to_broadcast([4, 4, S // 4]))
+
+        def load_column(name, src):
+            tile = keep.tile([P, PACK], F32, name=name)
+            nc.gpsimd.dma_start(tile[:], src.rearrange("(p t) o -> p (t o)", t=PACK))
+            return tile
+
+        def deal(engine_copy, name, raw, dtype):
+            tile = keep.tile([P, PACK, P], dtype, name=name, align_bytes=64)
+            engine_copy(tile[:].rearrange("p t m -> p m t"), raw[:].rearrange("p (m t) -> p m t", t=PACK))
+            return tile
+
+        def rows(name, dtype=F32, tag=None):
+            return [keep.tile([P, S], dtype, name=f"{name}{t}", tag=f"{tag or name}{t}") for t in tiles]
+
+        x_sc = keep.tile([P, TOKENS], U8, name="x_sc", align_bytes=64)
+        ws_a = keep.tile([P, S], U8, name="ws_a", align_bytes=64)
+        ws_b = keep.tile([P, S], U8, name="ws_b", align_bytes=64)
+
+        for q in range(4):
+            four_rows = x_scales[0, 4 * q : 4 * q + 4, :].bitcast(I32)
+            nc.sync.dma_start(x_sc[32 * q : 32 * q + 32, :].bitcast(I32), four_rows.unsqueeze(0).to_broadcast([8, 4, TOKENS // 4]))
+        l_two = load_list("l_two", two)
+        x_w = load_words("x_w", x_words, TOKENS)
+        w2_raw = load_words("w2_raw", w2_words, S)
+        l_offs = load_list("l_offs", offs)
+        load_scale_rows(nc.sync, ws_a, w2_scales, 0)
+        load_scale_rows(nc.sync, ws_a, w1_scales, 4)
+        w1_raw = load_words("w1_raw", w1_words, S)
+        l_three = load_list("l_three", three)
+        w3_raw = load_words("w3_raw", w3_words, S)
+        load_scale_rows(nc.sync, ws_b, w3_scales, 0)
+        l1 = load_list("l1", n1)
+        l2 = load_list("l2", n2)
+        l3 = load_list("l3", n3)
+        w4_raw = load_words("w4_raw", w4_words, S)
+        l4 = load_list("l4", n4)
+        l5 = load_list("l5", n5)
+        l6 = load_list("l6", n6)
+        l7 = load_list("l7", n7)
+        load_scale_rows(nc.gpsimd, ws_b, w4_scales, 4)
+        tau_c = load_column("tau_c", tau)
+        gn_c = load_column("gn_c", gn)
+        sl_c = load_column("sl_c", sl)
+        th_c = load_column("th_c", th)
+
+        def pick_scales(name, lst):
+            tile = keep.tile([P, S], U8, name=name, align_bytes=64)
+            nc.vector.tensor_copy(tile[:], x_sc[:].indirect(lst[:]))
+            return tile
+
+        def pick_words(name, lst):
+            tile = keep.tile([P, S], U32, name=name, align_bytes=64)
+            nc.vector.tensor_copy(tile[:], x_w[:].indirect(lst[:]))
+            return tile
+
+        def product(name, tag, w, w_sc, row, codes, scales, width):
+            banks = []
+            for t in tiles:
+                bank = psum.tile([P, S], F32, name=f"{name}{t}", tag=f"{tag}{t}")
+                nc.tensor.matmul_mx(
+                    out=bank[:, :width], lhsT=w[:, t, :].bitcast(FP8X4), lhsT_scale=w_sc[row:P, t, :],
+                    rhs=codes.bitcast(FP8X4), rhs_scale=scales, start=True, stop=True,
+                )
+                banks.append(bank)
+            return banks
+
+        xs_two = pick_scales("xs_two", l_two)
+        xs_offs = pick_scales("xs_offs", l_offs)
+        w2 = deal(nc.scalar.copy, "w2", w2_raw, U32)
+        wsc_a = deal(nc.vector.tensor_copy, "wsc_a", ws_a, U8)
+        xw_two = pick_words("xw_two", l_two)
+        w1 = deal(nc.scalar.copy, "w1", w1_raw, U32)
+        d_ps = product("d_ps", "pa", w2, wsc_a, 0, xw_two[:], xs_two[:], S)
+        w3 = deal(nc.scalar.copy, "w3", w3_raw, U32)
+        ad = rows("ad")
+        ad_twin = rows("ad_twin")
+        for t in tiles:
+            nc.scalar.activation(ad[t][:], d_ps[t][:], ACT.Abs)
+            nc.sync.dma_start(ad_twin[t][:], ad[t][:])
+
+        xw_offs = pick_words("xw_offs", l_offs)
+        y_ps = product("y_ps", "pb", w1, wsc_a, 4, xw_offs[:], xs_offs[:], S)
+        xs_three = pick_scales("xs_three", l_three)
+        y = rows("y")
+        num = rows("num")
+        for t in tiles:
+            if t < 2:
+                nc.scalar.copy(y[t][:], y_ps[t][:])
+            else:
+                nc.vector.tensor_copy(y[t][:], y_ps[t][:])
+            for hf in halves:
+                nc.scalar.activation(num[t][:, cols(hf)], y[t][:].indirect(part(l1, hf)), ACT.Copy)
+
+        xw_three = pick_words("xw_three", l_three)
+        wsc_b = deal(nc.vector.tensor_copy, "wsc_b", ws_b, U8)
+        b_ps = product("b_ps", "pa", w3, wsc_b, 0, xw_three[:], xs_three[:], S)
+        b = rows("b")
+        ea = rows("ea")
+        top = keep.tile([P, PACK], F32, name="top")
+        ea_bias = keep.tile([P, PACK], F32, name="ea_bias")
+        for t in tiles:
+            c = slice(t, t + 1)
+            nc.vector.tensor_scalar(b[t][:], b_ps[t][:], 1.0, None, ALU.mult, ALU.max, accum_out=top[:, c])
+            nc.vector.tensor_scalar(ea_bias[:, c], top[:, c], tau_c[:, c], -1.0, ALU.mult, ALU.mult)
+            for hf in halves:
+                nc.scalar.activation(ea[t][:, cols(hf)], b[t][:].indirect(part(l3, hf)), ACT.Exp, bias=ea_bias[:, c], scale=tau_c[:, c])
+
+        den = rows("den")
+        for t in tiles:
+            for hf in halves:
+                nc.vector.tensor_tensor(den[t][:, cols(hf)], ad[t][:].indirect(part(l2, hf)), ad_twin[t][:, cols(hf)], ALU.add)
+            nc.scalar.activation(den[t][:], den[t][:], ACT.Square, bias=0.5)
+        for t in tiles:
+            nc.vector.tensor_tensor(num[t][:], y[t][:], num[t][:], ALU.subtract)
+
+        gn_twice = keep.tile([P, PACK], F32, name="gn_twice")
+        nc.gpsimd.tensor_scalar(gn_twice[:], gn_c[:], 2.0, 0.0, ALU.mult, ALU.add)
+        gn_half = keep.tile([P, PACK], F32, name="gn_half")
+        nc.gpsimd.tensor_scalar(gn_half[:], gn_c[:], -0.5, 0.0, ALU.mult, ALU.add)
+        sg_bias = keep.tile([P, PACK], F32, name="sg_bias")
+        nc.gpsimd.tensor_tensor(sg_bias[:], sl_c[:], th_c[:], ALU.mult)
+        nc.gpsimd.tensor_scalar(sg_bias[:], sg_bias[:], -1.0, 0.0, ALU.mult, ALU.add)
+
+        m1 = rows("m1")
+        for t in tiles:
+            inv = keep.tile([P, S], F32, name=f"inv{t}", tag=f"b{PACK - 1 - t}")
+            nc.scalar.activation(inv[:], den[t][:], ACT.Abs_reciprocal_sqrt)
+            nc.vector.tensor_tensor(m1[t][:], num[t][:], inv[:], ALU.mult)
+        w4 = deal(nc.scalar.copy, "w4", w4_raw, U32)
+
+        def interleave(copy, name, src):
+            tile = keep.tile([P, HALF, PACK], BF16, name=name, align_bytes=64)
+            copy(tile[:].rearrange("p (c i) t -> p c t i", i=4), src[:].rearrange("p t (c i) -> p c t i", i=4))
+            return tile
+
+        h = rows("h")
+        own = rows("own")
+        for hf in halves:
+            z = keep.tile([P, PACK, HALF], BF16, name=f"z{hf}")
+            for t in tiles:
+                c = slice(t, t + 1)
+                u = keep.tile([P, HALF], F32, name=f"u{hf}{t}")
+                nc.scalar.activation(u[:], m1[t][:].indirect(part(l4, hf)), ACT.Copy)
+                nc.vector.tensor_tensor(u[:], m1[t][:, cols(hf)], u[:], ALU.subtract)
+                nc.vector.scalar_tensor_tensor(u[:], u[:], gn_twice[:, c], ea[t][:, cols(hf)], ALU.mult, ALU.mult)
+                nc.vector.scalar_tensor_tensor(z[:, t, :], b_ps[t][:, cols(hf)], gn_half[:, c], u[:], ALU.mult, ALU.add)
+            z_grouped = interleave(nc.vector.tensor_copy, f"z_grouped{hf}", z)
+            z_codes = keep.tile([P, HALF], U32, name=f"z_codes{hf}", align_bytes=64)
+            z_scales = keep.tile([P, HALF], U8, name=f"z_scales{hf}", align_bytes=64)
+            nc.vector.quantize_mx(out=z_codes[:].bitcast(FP8X4), scales=z_scales[:], in_=z_grouped[:].rearrange("p j t -> p (j t)"))
+            h_ps = product(f"h_ps{hf}", "pb" if hf == 0 else "pa", w4, wsc_b, 4, z_codes[:], z_scales[:], HALF)
+            for t in tiles:
+                c = slice(t, t + 1)
+                if hf == 0:
+                    nc.scalar.copy(h[t][:, cols(hf)], h_ps[t][:, :HALF])
+                else:
+                    nc.vector.tensor_copy(h[t][:, cols(hf)], h_ps[t][:, :HALF])
+                nc.scalar.activation(own[t][:, cols(hf)], h[t][:, cols(hf)], ACT.Sigmoid, bias=sg_bias[:, c], scale=sl_c[:, c])
+
+        out_rows = out_0.rearrange("(p t) j -> p t j", t=PACK)
+        out_words = out_1[0].rearrange("p n t -> p (n t)").bitcast(I32)
+        o_scales = keep.tile([P, S], U8, name="o_scales", align_bytes=64)
+        for hf in halves:
+            sg = keep.tile([P, PACK, HALF], F32, name=f"sg{hf}")
+            h7 = keep.tile([P, PACK, HALF], F32, name=f"h7{hf}")
+            res = keep.tile([P, PACK, HALF], F32, name=f"res{hf}")
+            for pair in range(2):
+                both = slice(2 * pair, 2 * pair + 2)
+                for t in (2 * pair, 2 * pair + 1):
+                    c = slice(t, t + 1)
+                    nc.scalar.activation(sg[:, t, :], h[t][:].indirect(part(l5, hf)), ACT.Sigmoid, bias=sg_bias[:, c], scale=sl_c[:, c])
+                    nc.scalar.activation(h7[:, t, :], h[t][:].indirect(part(l7, hf)), ACT.Copy)
+                    nc.vector.tensor_tensor(res[:, t, :], h[t][:].indirect(part(l6, hf)), own[t][:, cols(hf)], ALU.mult)
+                nc.vector.tensor_tensor(sg[:, both, :], sg[:, both, :], h7[:, both, :], ALU.mult)
+                nc.vector.tensor_tensor(res[:, both, :], res[:, both, :], sg[:, both, :], ALU.add)
+                nc.sync.dma_start(out_rows[:, both, cols(hf)], res[:, both, :])
+            o_grouped = interleave(nc.scalar.copy if hf == 0 else nc.vector.tensor_copy, f"o_grouped{hf}", res)
+            o_codes = keep.tile([P, HALF], U32, name=f"o_codes{hf}", align_bytes=64)
+            nc.vector.quantize_mx(out=o_codes[:].bitcast(FP8X4), scales=o_scales[:, cols(hf)], in_=o_grouped[:].rearrange("p j t -> p (j t)"))
+            nc.sync.dma_start(out_words[:, cols(hf)], o_codes[:].bitcast(I32))
+        for q in range(4):
+            queue = nc.sync if q % 2 else nc.scalar
+            queue.dma_start(out_2[0, 4 * q : 4 * q + 4, :].bitcast(I32), o_scales[32 * q : 32 * q + 4, :].bitcast(I32))

@@ -18,6 +18,8 @@ TOKENS = 2048
 S = 512
 HALF = S // 2
 LIST_COLS = S // 16
+SCALAR_SHARE = 96
+SPARE = 16
 FLOPS = 4 * 2 * 512 * 512 * 512
 
 
@@ -41,8 +43,8 @@ def tile_picked_trionormbpxbemx_none_po_kernel(
             nc.sync.dma_start(tile[:], src)
             return tile
 
-        def part(lst, half):
-            return lst[:, half * LIST_COLS // 2 : (half + 1) * LIST_COLS // 2]
+        def part(lst, j):
+            return lst[:, j.start // 16 : j.stop // 16]
 
         def load_words(name, src, width):
             tile = keep.tile([P, width], U32, name=name, align_bytes=64)
@@ -59,53 +61,69 @@ def tile_picked_trionormbpxbemx_none_po_kernel(
             nc.gpsimd.dma_start(tile[:], src.rearrange("(p t) o -> p (t o)", t=PACK))
             return tile
 
-        def deal(engine_copy, name, raw, dtype):
-            tile = keep.tile([P, PACK, P], dtype, name=name, align_bytes=64)
+        def deal(engine_copy, name, raw, dtype, tag=None):
+            tile = keep.tile([P, PACK, P], dtype, name=name, tag=tag or name, align_bytes=64)
             engine_copy(tile[:].rearrange("p t m -> p m t"), raw[:].rearrange("p (m t) -> p m t", t=PACK))
             return tile
 
         def rows(name, dtype=F32, tag=None):
-            return [keep.tile([P, S], dtype, name=f"{name}{t}", tag=f"{tag or name}{t}") for t in tiles]
+            return [keep.tile([P, S], dtype, name=f"{name}{t}", tag=f"{tag or name}{t}", align_bytes=64) for t in tiles]
 
-        x_sc = keep.tile([P, TOKENS], U8, name="x_sc", align_bytes=64)
-        ws_a = keep.tile([P, S], U8, name="ws_a", align_bytes=64)
-        ws_b = keep.tile([P, S], U8, name="ws_b", align_bytes=64)
+        def load_plane(queue, name, src, width):
+            tile = keep.tile([P, width], U8, name=name, tag=name, align_bytes=64)
+            for q in range(4):
+                four_rows = src[0, 4 * q : 4 * q + 4, :].bitcast(I32)
+                queue.dma_start(tile[32 * q : 32 * q + 32, :].bitcast(I32), four_rows.unsqueeze(0).to_broadcast([8, 4, width // 4]))
+            return tile
 
-        for q in range(4):
-            four_rows = x_scales[0, 4 * q : 4 * q + 4, :].bitcast(I32)
-            nc.sync.dma_start(x_sc[32 * q : 32 * q + 32, :].bitcast(I32), four_rows.unsqueeze(0).to_broadcast([8, 4, TOKENS // 4]))
+        def windows(name, width):
+            made = [keep.tile([P, width], F32, name=f"{name}{t}", tag=f"{name}{t}", align_bytes=64) for t in tiles]
+            for tile in made:
+                nc.vector.memset(tile[:, S:], 0.0)
+            return made
+
+        y = windows("y", S + SPARE)
+        ad = windows("ad", S + SPARE)
+        wide = windows("wide", 2 * S)
+        m1 = windows("m1", S + SPARE)
+
         l_two = load_list("l_two", two)
+        l_offs = load_list("l_offs", offs)
+        x_sc = load_plane(nc.sync, "x_sc", x_scales, TOKENS)
         x_w = load_words("x_w", x_words, TOKENS)
         w2_raw = load_words("w2_raw", w2_words, S)
-        l_offs = load_list("l_offs", offs)
-        load_scale_rows(nc.sync, ws_a, w2_scales, 0)
-        load_scale_rows(nc.sync, ws_a, w1_scales, 4)
-        w1_raw = load_words("w1_raw", w1_words, S)
+        ws2_raw = load_plane(nc.sync, "ws2_raw", w2_scales, S)
         l_three = load_list("l_three", three)
-        w3_raw = load_words("w3_raw", w3_words, S)
-        load_scale_rows(nc.sync, ws_b, w3_scales, 0)
+        w1_raw = load_words("w1_raw", w1_words, S)
+        ws14_raw = keep.tile([P, S], U8, name="ws14_raw", tag="ws14_raw", align_bytes=64)
+        load_scale_rows(nc.sync, ws14_raw, w1_scales, 0)
         l1 = load_list("l1", n1)
+        w3_raw = load_words("w3_raw", w3_words, S)
         l2 = load_list("l2", n2)
+        ws3_raw = load_plane(nc.sync, "ws3_raw", w3_scales, S)
         l3 = load_list("l3", n3)
         w4_raw = load_words("w4_raw", w4_words, S)
         l4 = load_list("l4", n4)
         l5 = load_list("l5", n5)
         l6 = load_list("l6", n6)
         l7 = load_list("l7", n7)
-        load_scale_rows(nc.gpsimd, ws_b, w4_scales, 4)
+        load_scale_rows(nc.gpsimd, ws14_raw, w4_scales, 4)
         tau_c = load_column("tau_c", tau)
         gn_c = load_column("gn_c", gn)
         sl_c = load_column("sl_c", sl)
         th_c = load_column("th_c", th)
 
-        def pick_scales(name, lst):
-            tile = keep.tile([P, S], U8, name=name, align_bytes=64)
-            nc.vector.tensor_copy(tile[:], x_sc[:].indirect(lst[:]))
-            return tile
+        gn_twice = keep.tile([P, PACK], F32, name="gn_twice")
+        nc.gpsimd.tensor_scalar(gn_twice[:], gn_c[:], 2.0, 0.0, ALU.mult, ALU.add)
+        gn_half = keep.tile([P, PACK], F32, name="gn_half")
+        nc.gpsimd.tensor_scalar(gn_half[:], gn_c[:], -0.5, 0.0, ALU.mult, ALU.add)
+        sg_bias = keep.tile([P, PACK], F32, name="sg_bias")
+        nc.gpsimd.tensor_tensor(sg_bias[:], sl_c[:], th_c[:], ALU.mult)
+        nc.gpsimd.tensor_scalar(sg_bias[:], sg_bias[:], -1.0, 0.0, ALU.mult, ALU.add)
 
-        def pick_words(name, lst):
-            tile = keep.tile([P, S], U32, name=name, align_bytes=64)
-            nc.vector.tensor_copy(tile[:], x_w[:].indirect(lst[:]))
+        def pick(name, table, dtype, lst, tag=None):
+            tile = keep.tile([P, S], dtype, name=name, tag=tag or name, align_bytes=64)
+            nc.vector.tensor_copy(tile[:], table[:].indirect(lst[:]))
             return tile
 
         def product(name, tag, w, w_sc, row, codes, scales, width):
@@ -119,120 +137,169 @@ def tile_picked_trionormbpxbemx_none_po_kernel(
                 banks.append(bank)
             return banks
 
-        xs_two = pick_scales("xs_two", l_two)
-        xs_offs = pick_scales("xs_offs", l_offs)
+        xs_two = pick("xs_two", x_sc, U8, l_two)
+        xs_offs = pick("xs_offs", x_sc, U8, l_offs)
         w2 = deal(nc.scalar.copy, "w2", w2_raw, U32)
-        wsc_a = deal(nc.vector.tensor_copy, "wsc_a", ws_a, U8)
-        xw_two = pick_words("xw_two", l_two)
+        ws2 = deal(nc.vector.tensor_copy, "ws2", ws2_raw, U8)
+        xw_two = pick("xw_two", x_w, U32, l_two)
         w1 = deal(nc.scalar.copy, "w1", w1_raw, U32)
-        d_ps = product("d_ps", "pa", w2, wsc_a, 0, xw_two[:], xs_two[:], S)
-        w3 = deal(nc.scalar.copy, "w3", w3_raw, U32)
-        ad = rows("ad")
+        d_ps = product("d_ps", "pa", w2, ws2, 0, xw_two[:], xs_two[:], S)
         ad_twin = rows("ad_twin")
         for t in tiles:
-            nc.scalar.activation(ad[t][:], d_ps[t][:], ACT.Abs)
-            nc.sync.dma_start(ad_twin[t][:], ad[t][:])
+            nc.scalar.activation(ad[t][:, :S], d_ps[t][:], ACT.Abs)
+            nc.sync.dma_start(ad_twin[t][:], ad[t][:, :S])
 
-        xw_offs = pick_words("xw_offs", l_offs)
-        y_ps = product("y_ps", "pb", w1, wsc_a, 4, xw_offs[:], xs_offs[:], S)
-        xs_three = pick_scales("xs_three", l_three)
-        y = rows("y")
-        num = rows("num")
-        for t in tiles:
-            if t < 2:
-                nc.scalar.copy(y[t][:], y_ps[t][:])
-            else:
-                nc.vector.tensor_copy(y[t][:], y_ps[t][:])
-            for hf in halves:
-                nc.scalar.activation(num[t][:, cols(hf)], y[t][:].indirect(part(l1, hf)), ACT.Copy)
+        xw_offs = pick("xw_offs", x_w, U32, l_offs, tag="ws2_raw")
+        xs_three = pick("xs_three", x_sc, U8, l_three)
+        ws14 = deal(nc.vector.tensor_copy, "ws14", ws14_raw, U8)
+        y_ps = product("y_ps", "pb", w1, ws14, 0, xw_offs[:], xs_offs[:], S)
+        y_at = rows("y_at")
 
-        xw_three = pick_words("xw_three", l_three)
-        wsc_b = deal(nc.vector.tensor_copy, "wsc_b", ws_b, U8)
-        b_ps = product("b_ps", "pa", w3, wsc_b, 0, xw_three[:], xs_three[:], S)
-        b = rows("b")
+        def look_up_y(t, copy):
+            copy(y[t][:, :S], y_ps[t][:])
+            nc.scalar.activation(y_at[t][:], y[t][:].indirect(l1[:]), ACT.Copy)
+
+        look_up_y(0, nc.scalar.copy)
+        look_up_y(1, nc.vector.tensor_copy)
+
+        xw_three = pick("xw_three", x_w, U32, l_three, tag="ws14_raw")
+        w3 = keep.tile([P, PACK, P], U32, name="w3", tag="w3", align_bytes=64)
+        nc.vector.tensor_copy(w3[:].bitcast(I32).rearrange("p t m -> p m t"), w3_raw[:].bitcast(I32).rearrange("p (m t) -> p m t", t=PACK))
+        ws3 = deal(nc.vector.tensor_copy, "ws3", ws3_raw, U8)
+        b_ps = product("b_ps", "pa", w3, ws3, 0, xw_three[:], xs_three[:], S)
+        look_up_y(2, nc.vector.tensor_copy)
+        look_up_y(3, nc.vector.tensor_copy)
         ea = rows("ea")
         top = keep.tile([P, PACK], F32, name="top")
         ea_bias = keep.tile([P, PACK], F32, name="ea_bias")
         for t in tiles:
             c = slice(t, t + 1)
-            nc.vector.tensor_scalar(b[t][:], b_ps[t][:], 1.0, None, ALU.mult, ALU.max, accum_out=top[:, c])
-            nc.vector.tensor_scalar(ea_bias[:, c], top[:, c], tau_c[:, c], -1.0, ALU.mult, ALU.mult)
-            for hf in halves:
-                nc.scalar.activation(ea[t][:, cols(hf)], b[t][:].indirect(part(l3, hf)), ACT.Exp, bias=ea_bias[:, c], scale=tau_c[:, c])
+            nc.vector.tensor_scalar(wide[t][:, :S], b_ps[t][:], 1.0, None, ALU.mult, ALU.max, accum_out=top[:, c])
+            nc.gpsimd.tensor_scalar(ea_bias[:, c], top[:, c], tau_c[:, c], -1.0, ALU.mult, ALU.mult)
+            nc.scalar.activation(ea[t][:], wide[t][:].indirect(l3[:]), ACT.Exp, bias=ea_bias[:, c], scale=tau_c[:, c])
 
-        den = rows("den")
+        den = [keep.tile([P, S], F32, name=f"den{t}", tag=tag, align_bytes=64) for t, tag in enumerate(("ws14_raw", "w3", "xs_three", "ws3"))]
         for t in tiles:
-            for hf in halves:
-                nc.vector.tensor_tensor(den[t][:, cols(hf)], ad[t][:].indirect(part(l2, hf)), ad_twin[t][:, cols(hf)], ALU.add)
-            nc.scalar.activation(den[t][:], den[t][:], ACT.Square, bias=0.5)
-        for t in tiles:
-            nc.vector.tensor_tensor(num[t][:], y[t][:], num[t][:], ALU.subtract)
+            nc.vector.tensor_tensor(den[t][:], ad[t][:].indirect(l2[:]), ad_twin[t][:], ALU.add)
+        num = rows("diff", tag="ad")
 
-        gn_twice = keep.tile([P, PACK], F32, name="gn_twice")
-        nc.gpsimd.tensor_scalar(gn_twice[:], gn_c[:], 2.0, 0.0, ALU.mult, ALU.add)
-        gn_half = keep.tile([P, PACK], F32, name="gn_half")
-        nc.gpsimd.tensor_scalar(gn_half[:], gn_c[:], -0.5, 0.0, ALU.mult, ALU.add)
-        sg_bias = keep.tile([P, PACK], F32, name="sg_bias")
-        nc.gpsimd.tensor_tensor(sg_bias[:], sl_c[:], th_c[:], ALU.mult)
-        nc.gpsimd.tensor_scalar(sg_bias[:], sg_bias[:], -1.0, 0.0, ALU.mult, ALU.add)
+        def make_num(t):
+            nc.vector.tensor_tensor(num[t][:], y[t][:, :S], y_at[t][:], ALU.subtract)
 
-        m1 = rows("m1")
-        for t in tiles:
-            inv = keep.tile([P, S], F32, name=f"inv{t}", tag=f"b{PACK - 1 - t}")
-            nc.scalar.activation(inv[:], den[t][:], ACT.Abs_reciprocal_sqrt)
-            nc.vector.tensor_tensor(m1[t][:], num[t][:], inv[:], ALU.mult)
-        w4 = deal(nc.scalar.copy, "w4", w4_raw, U32)
+        u = rows("u")
+        z = keep.tile([P, PACK, S], BF16, name="z")
 
-        def interleave(copy, name, src):
+        def make_m1(t):
+            inv = wide[PACK - 1 - t][:, :S]
+            nc.scalar.activation(inv, den[t][:], ACT.Square, bias=0.5)
+            nc.scalar.activation(inv, inv, ACT.Abs_reciprocal_sqrt)
+            nc.vector.tensor_tensor(m1[t][:, :S], num[t][:], inv, ALU.mult)
+
+        def look_up_m1(t, j):
+            nc.scalar.activation(u[t][:, j], m1[t][:].indirect(part(l4, j)), ACT.Copy)
+
+        def subtract_m1(t, j):
+            nc.vector.tensor_tensor(u[t][:, j], m1[t][:, j], u[t][:, j], ALU.subtract)
+
+        def weigh(t, j):
+            nc.vector.scalar_tensor_tensor(u[t][:, j], u[t][:, j], gn_twice[:, t : t + 1], ea[t][:, j], ALU.mult, ALU.mult)
+
+        def make_z(t, j):
+            nc.vector.scalar_tensor_tensor(z[:, t, j], b_ps[t][:, j], gn_half[:, t : t + 1], u[t][:, j], ALU.mult, ALU.add)
+
+        def interleave(name, src, on_scalar):
             tile = keep.tile([P, HALF, PACK], BF16, name=name, align_bytes=64)
-            copy(tile[:].rearrange("p (c i) t -> p c t i", i=4), src[:].rearrange("p t (c i) -> p c t i", i=4))
+            for copy, a, e in ((nc.scalar.copy, 0, on_scalar), (nc.vector.tensor_copy, on_scalar, HALF)):
+                if e > a:
+                    copy(tile[:, a:e, :].rearrange("p (c i) t -> p c t i", i=4), src[:, :, a:e].rearrange("p t (c i) -> p c t i", i=4))
             return tile
 
-        h = rows("h")
+        h = wide
         own = rows("own")
-        for hf in halves:
-            z = keep.tile([P, PACK, HALF], BF16, name=f"z{hf}")
-            for t in tiles:
-                c = slice(t, t + 1)
-                u = keep.tile([P, HALF], F32, name=f"u{hf}{t}")
-                nc.scalar.activation(u[:], m1[t][:].indirect(part(l4, hf)), ACT.Copy)
-                nc.vector.tensor_tensor(u[:], m1[t][:, cols(hf)], u[:], ALU.subtract)
-                nc.vector.scalar_tensor_tensor(u[:], u[:], gn_twice[:, c], ea[t][:, cols(hf)], ALU.mult, ALU.mult)
-                nc.vector.scalar_tensor_tensor(z[:, t, :], b_ps[t][:, cols(hf)], gn_half[:, c], u[:], ALU.mult, ALU.add)
-            z_grouped = interleave(nc.vector.tensor_copy, f"z_grouped{hf}", z)
+
+        def make_h(hf, on_scalar, tag):
+            z_grouped = interleave(f"z_grouped{hf}", z[:, :, cols(hf)], on_scalar)
             z_codes = keep.tile([P, HALF], U32, name=f"z_codes{hf}", align_bytes=64)
             z_scales = keep.tile([P, HALF], U8, name=f"z_scales{hf}", align_bytes=64)
             nc.vector.quantize_mx(out=z_codes[:].bitcast(FP8X4), scales=z_scales[:], in_=z_grouped[:].rearrange("p j t -> p (j t)"))
-            h_ps = product(f"h_ps{hf}", "pb" if hf == 0 else "pa", w4, wsc_b, 4, z_codes[:], z_scales[:], HALF)
-            for t in tiles:
-                c = slice(t, t + 1)
-                if hf == 0:
-                    nc.scalar.copy(h[t][:, cols(hf)], h_ps[t][:, :HALF])
-                else:
-                    nc.vector.tensor_copy(h[t][:, cols(hf)], h_ps[t][:, :HALF])
-                nc.scalar.activation(own[t][:, cols(hf)], h[t][:, cols(hf)], ACT.Sigmoid, bias=sg_bias[:, c], scale=sl_c[:, c])
+            return product(f"h_ps{hf}", tag, w4, ws14, 4, z_codes[:], z_scales[:], HALF)
+
+        def make_own(hf, t, src):
+            nc.scalar.activation(own[t][:, cols(hf)], src, ACT.Sigmoid, bias=sg_bias[:, t : t + 1], scale=sl_c[:, t : t + 1])
+
+        whole = slice(0, S)
+        make_num(0)
+        make_num(1)
+        make_m1(0)
+        make_num(2)
+        make_m1(1)
+        make_num(3)
+        look_up_m1(0, whole)
+        subtract_m1(0, whole)
+        weigh(0, whole)
+        make_m1(2)
+        make_z(0, whole)
+        look_up_m1(1, whole)
+        subtract_m1(1, whole)
+        weigh(1, whole)
+        make_m1(3)
+        make_z(1, whole)
+        for hf in halves:
+            for t in (2, 3):
+                look_up_m1(t, cols(hf))
+        w4 = deal(nc.scalar.copy, "w4", w4_raw, U32, tag="m10")
+        for step in (subtract_m1, weigh, make_z):
+            for t in (2, 3):
+                step(t, cols(0))
+        for step in (subtract_m1, weigh):
+            for t in (2, 3):
+                step(t, cols(1))
+        h_first = make_h(0, HALF, "pb")
+        for t in tiles:
+            make_own(0, t, h_first[t][:, :HALF])
+        for t in (0, 1):
+            nc.scalar.copy(h[t][:, cols(0)], h_first[t][:, :HALF])
+        for t in (2, 3):
+            make_z(t, cols(1))
+        h_second = make_h(1, 0, "pa")
+        for t in (2, 3):
+            nc.vector.tensor_copy(h[t][:, cols(0)], h_first[t][:, :HALF])
+        for t in tiles:
+            (nc.scalar.copy if t == 0 else nc.vector.tensor_copy)(h[t][:, cols(1)], h_second[t][:, :HALF])
 
         out_rows = out_0.rearrange("(p t) j -> p t j", t=PACK)
         out_words = out_1[0].rearrange("p n t -> p (n t)").bitcast(I32)
         o_scales = keep.tile([P, S], U8, name="o_scales", align_bytes=64)
-        for hf in halves:
-            sg = keep.tile([P, PACK, HALF], F32, name=f"sg{hf}")
-            h7 = keep.tile([P, PACK, HALF], F32, name=f"h7{hf}")
-            res = keep.tile([P, PACK, HALF], F32, name=f"res{hf}")
-            for pair in range(2):
-                both = slice(2 * pair, 2 * pair + 2)
-                for t in (2 * pair, 2 * pair + 1):
-                    c = slice(t, t + 1)
-                    nc.scalar.activation(sg[:, t, :], h[t][:].indirect(part(l5, hf)), ACT.Sigmoid, bias=sg_bias[:, c], scale=sl_c[:, c])
-                    nc.scalar.activation(h7[:, t, :], h[t][:].indirect(part(l7, hf)), ACT.Copy)
-                    nc.vector.tensor_tensor(res[:, t, :], h[t][:].indirect(part(l6, hf)), own[t][:, cols(hf)], ALU.mult)
-                nc.vector.tensor_tensor(sg[:, both, :], sg[:, both, :], h7[:, both, :], ALU.mult)
-                nc.vector.tensor_tensor(res[:, both, :], res[:, both, :], sg[:, both, :], ALU.add)
-                nc.sync.dma_start(out_rows[:, both, cols(hf)], res[:, both, :])
-            o_grouped = interleave(nc.scalar.copy if hf == 0 else nc.vector.tensor_copy, f"o_grouped{hf}", res)
+        sg = rows("sg")
+        h7 = rows("h7")
+        res = keep.tile([P, PACK, S], F32, name="res")
+
+        def finish(t, j):
+            nc.vector.tensor_tensor(res[:, t, j], res[:, t, j], sg[t][:, j], ALU.add)
+            nc.sync.dma_start(out_rows[:, t, j], res[:, t, j])
+
+        def hand_on(hf, grouped):
             o_codes = keep.tile([P, HALF], U32, name=f"o_codes{hf}", align_bytes=64)
-            nc.vector.quantize_mx(out=o_codes[:].bitcast(FP8X4), scales=o_scales[:, cols(hf)], in_=o_grouped[:].rearrange("p j t -> p (j t)"))
+            nc.vector.quantize_mx(out=o_codes[:].bitcast(FP8X4), scales=o_scales[:, cols(hf)], in_=grouped[:].rearrange("p j t -> p (j t)"))
             nc.sync.dma_start(out_words[:, cols(hf)], o_codes[:].bitcast(I32))
+
+        last = PACK - 1
+        steps = [(t, whole) for t in range(last)] + [(last, cols(hf)) for hf in halves]
+        for i, (t, j) in enumerate(steps):
+            c = slice(t, t + 1)
+            if j != cols(1):
+                make_own(1, t, h[t][:, cols(1)])
+            nc.scalar.activation(sg[t][:, j], h[t][:].indirect(part(l5, j)), ACT.Sigmoid, bias=sg_bias[:, c], scale=sl_c[:, c])
+            nc.scalar.activation(h7[t][:, j], h[t][:].indirect(part(l7, j)), ACT.Copy)
+            nc.vector.tensor_tensor(res[:, t, j], h[t][:].indirect(part(l6, j)), own[t][:, j], ALU.mult)
+            if i > 0:
+                finish(*steps[i - 1])
+            if j == cols(1):
+                grouped = interleave("o_grouped0", res[:, :, cols(0)], 0)
+            nc.vector.tensor_tensor(sg[t][:, j], sg[t][:, j], h7[t][:, j], ALU.mult)
+        hand_on(0, grouped)
+        finish(*steps[-1])
+        hand_on(1, interleave("o_grouped1", res[:, :, cols(1)], SCALAR_SHARE))
         for q in range(4):
             queue = nc.sync if q % 2 else nc.scalar
             queue.dma_start(out_2[0, 4 * q : 4 * q + 4, :].bitcast(I32), o_scales[32 * q : 32 * q + 4, :].bitcast(I32))

@@ -47,18 +47,22 @@ def tile_picked_trionormbpxbemx_none_po_kernel(
             return lst[:, j.start // 16 : j.stop // 16]
 
         def load_words(name, src, width):
-            tile = keep.tile([P, width], U32, name=name, align_bytes=64)
+            tile = keep.tile([P, width], U32, name=name, tag=name, align_bytes=64)
             nc.sync.dma_start(tile[:].bitcast(I32), src[0].rearrange("p n t -> p (n t)").bitcast(I32))
             return tile
 
-        def load_scale_rows(queue, tile, src, row):
-            for r in range(4):
-                every_fourth = src[0, r::4, :].bitcast(I32)
-                queue.dma_start(tile[row + r :: 8, :].bitcast(I32), every_fourth.unsqueeze(1).to_broadcast([4, 4, S // 4]))
+        def scale_tile(name, width):
+            tile = keep.tile([P, width], U8, name=name, tag=name, align_bytes=64)
+            nc.vector.memset(tile[:].bitcast(I32), 0)
+            return tile
+
+        def load_scale_rows(tile, src, row):
+            for q in range(4):
+                nc.sync.dma_start(tile[32 * q + row : 32 * q + row + 4, :].bitcast(I32), src[0, 4 * q : 4 * q + 4, :].bitcast(I32))
 
         def load_column(name, src):
             tile = keep.tile([P, PACK], F32, name=name)
-            nc.gpsimd.dma_start(tile[:], src.rearrange("(p t) o -> p (t o)", t=PACK))
+            nc.sync.dma_start(tile[:], src.rearrange("(p t) o -> p (t o)", t=PACK))
             return tile
 
         def deal(engine_copy, name, raw, dtype, tag=None):
@@ -69,57 +73,37 @@ def tile_picked_trionormbpxbemx_none_po_kernel(
         def rows(name, dtype=F32, tag=None):
             return [keep.tile([P, S], dtype, name=f"{name}{t}", tag=f"{tag or name}{t}", align_bytes=64) for t in tiles]
 
-        def load_plane(queue, name, src, width):
-            tile = keep.tile([P, width], U8, name=name, tag=name, align_bytes=64)
-            for q in range(4):
-                four_rows = src[0, 4 * q : 4 * q + 4, :].bitcast(I32)
-                queue.dma_start(tile[32 * q : 32 * q + 32, :].bitcast(I32), four_rows.unsqueeze(0).to_broadcast([8, 4, width // 4]))
-            return tile
-
-        def windows(name, width):
-            made = [keep.tile([P, width], F32, name=f"{name}{t}", tag=f"{name}{t}", align_bytes=64) for t in tiles]
+        def windows(name, spare):
+            made = [keep.tile([P, S + spare], F32, name=f"{name}{t}", tag=f"{name}{t}", align_bytes=64) for t in tiles]
             for tile in made:
                 nc.vector.memset(tile[:, S:], 0.0)
             return made
 
-        y = windows("y", S + SPARE)
-        ad = windows("ad", S + SPARE)
-        wide = windows("wide", 2 * S)
-        m1 = windows("m1", S + SPARE)
+        x_sc = scale_tile("x_sc", TOKENS)
+        ws2_raw = scale_tile("ws2_raw", S)
+        ws3_raw = scale_tile("ws3_raw", S)
+        ws14_raw = scale_tile("ws14_raw", S)
+        ad = windows("ad", SPARE)
+        wide = windows("wide", S)
+        y = windows("y", SPARE)
+        m1 = windows("m1", SPARE)
 
         l_two = load_list("l_two", two)
-        l_offs = load_list("l_offs", offs)
-        x_sc = load_plane(nc.sync, "x_sc", x_scales, TOKENS)
+        l_three = load_list("l_three", three)
+        load_scale_rows(x_sc, x_scales, 0)
         x_w = load_words("x_w", x_words, TOKENS)
         w2_raw = load_words("w2_raw", w2_words, S)
-        ws2_raw = load_plane(nc.sync, "ws2_raw", w2_scales, S)
-        l_three = load_list("l_three", three)
-        w1_raw = load_words("w1_raw", w1_words, S)
-        ws14_raw = keep.tile([P, S], U8, name="ws14_raw", tag="ws14_raw", align_bytes=64)
-        load_scale_rows(nc.sync, ws14_raw, w1_scales, 0)
-        l1 = load_list("l1", n1)
+        load_scale_rows(ws2_raw, w2_scales, 0)
+        l_offs = load_list("l_offs", offs)
         w3_raw = load_words("w3_raw", w3_words, S)
-        l2 = load_list("l2", n2)
-        ws3_raw = load_plane(nc.sync, "ws3_raw", w3_scales, S)
-        l3 = load_list("l3", n3)
-        w4_raw = load_words("w4_raw", w4_words, S)
-        l4 = load_list("l4", n4)
-        l5 = load_list("l5", n5)
-        l6 = load_list("l6", n6)
-        l7 = load_list("l7", n7)
-        load_scale_rows(nc.gpsimd, ws14_raw, w4_scales, 4)
+        load_scale_rows(ws3_raw, w3_scales, 0)
         tau_c = load_column("tau_c", tau)
-        gn_c = load_column("gn_c", gn)
-        sl_c = load_column("sl_c", sl)
-        th_c = load_column("th_c", th)
-
-        gn_twice = keep.tile([P, PACK], F32, name="gn_twice")
-        nc.gpsimd.tensor_scalar(gn_twice[:], gn_c[:], 2.0, 0.0, ALU.mult, ALU.add)
-        gn_half = keep.tile([P, PACK], F32, name="gn_half")
-        nc.gpsimd.tensor_scalar(gn_half[:], gn_c[:], -0.5, 0.0, ALU.mult, ALU.add)
-        sg_bias = keep.tile([P, PACK], F32, name="sg_bias")
-        nc.gpsimd.tensor_tensor(sg_bias[:], sl_c[:], th_c[:], ALU.mult)
-        nc.gpsimd.tensor_scalar(sg_bias[:], sg_bias[:], -1.0, 0.0, ALU.mult, ALU.add)
+        l3 = load_list("l3", n3)
+        w1_raw = load_words("w1_raw", w1_words, S)
+        load_scale_rows(ws14_raw, w1_scales, 0)
+        load_scale_rows(ws14_raw, w4_scales, 4)
+        l2 = load_list("l2", n2)
+        l1 = load_list("l1", n1)
 
         def pick(name, table, dtype, lst, tag=None):
             tile = keep.tile([P, S], dtype, name=name, tag=tag or name, align_bytes=64)
@@ -138,50 +122,61 @@ def tile_picked_trionormbpxbemx_none_po_kernel(
             return banks
 
         xs_two = pick("xs_two", x_sc, U8, l_two)
-        xs_offs = pick("xs_offs", x_sc, U8, l_offs)
+        xs_three = pick("xs_three", x_sc, U8, l_three)
         w2 = deal(nc.scalar.copy, "w2", w2_raw, U32)
         ws2 = deal(nc.vector.tensor_copy, "ws2", ws2_raw, U8)
         xw_two = pick("xw_two", x_w, U32, l_two)
-        w1 = deal(nc.scalar.copy, "w1", w1_raw, U32)
+        w3 = deal(nc.scalar.copy, "w3", w3_raw, U32)
         d_ps = product("d_ps", "pa", w2, ws2, 0, xw_two[:], xs_two[:], S)
         ad_twin = rows("ad_twin")
         for t in tiles:
             nc.scalar.activation(ad[t][:, :S], d_ps[t][:], ACT.Abs)
             nc.sync.dma_start(ad_twin[t][:], ad[t][:, :S])
+        w1 = deal(nc.scalar.copy, "w1", w1_raw, U32)
 
-        xw_offs = pick("xw_offs", x_w, U32, l_offs, tag="ws2_raw")
-        xs_three = pick("xs_three", x_sc, U8, l_three)
-        ws14 = deal(nc.vector.tensor_copy, "ws14", ws14_raw, U8)
-        y_ps = product("y_ps", "pb", w1, ws14, 0, xw_offs[:], xs_offs[:], S)
-        y_at = rows("y_at")
+        gn_c = load_column("gn_c", gn)
+        l4 = load_list("l4", n4)
+        w4_raw = load_words("w4_raw", w4_words, S)
+        sl_c = load_column("sl_c", sl)
+        th_c = load_column("th_c", th)
+        l5 = load_list("l5", n5)
+        l6 = load_list("l6", n6)
+        l7 = load_list("l7", n7)
 
-        def look_up_y(t, copy):
-            copy(y[t][:, :S], y_ps[t][:])
-            nc.scalar.activation(y_at[t][:], y[t][:].indirect(l1[:]), ACT.Copy)
-
-        look_up_y(0, nc.scalar.copy)
-        look_up_y(1, nc.vector.tensor_copy)
-
-        xw_three = pick("xw_three", x_w, U32, l_three, tag="ws14_raw")
-        w3 = keep.tile([P, PACK, P], U32, name="w3", tag="w3", align_bytes=64)
-        nc.vector.tensor_copy(w3[:].bitcast(I32).rearrange("p t m -> p m t"), w3_raw[:].bitcast(I32).rearrange("p (m t) -> p m t", t=PACK))
+        xw_three = pick("xw_three", x_w, U32, l_three, tag="ws2_raw")
         ws3 = deal(nc.vector.tensor_copy, "ws3", ws3_raw, U8)
-        b_ps = product("b_ps", "pa", w3, ws3, 0, xw_three[:], xs_three[:], S)
-        look_up_y(2, nc.vector.tensor_copy)
-        look_up_y(3, nc.vector.tensor_copy)
+        b_ps = product("b_ps", "pb", w3, ws3, 0, xw_three[:], xs_three[:], S)
+        xs_offs = pick("xs_offs", x_sc, U8, l_offs, tag="ws3_raw")
         ea = rows("ea")
-        top = keep.tile([P, PACK], F32, name="top")
-        ea_bias = keep.tile([P, PACK], F32, name="ea_bias")
-        for t in tiles:
+        top = keep.tile([P, PACK], F32, name="top", tag="top")
+        ea_bias = keep.tile([P, PACK], F32, name="ea_bias", tag="ea_bias")
+
+        def look_up_b(t):
             c = slice(t, t + 1)
-            nc.vector.tensor_scalar(wide[t][:, :S], b_ps[t][:], 1.0, None, ALU.mult, ALU.max, accum_out=top[:, c])
-            nc.gpsimd.tensor_scalar(ea_bias[:, c], top[:, c], tau_c[:, c], -1.0, ALU.mult, ALU.mult)
+            nc.vector.tensor_scalar(ea_bias[:, c], top[:, c], tau_c[:, c], -1.0, ALU.mult, ALU.mult)
             nc.scalar.activation(ea[t][:], wide[t][:].indirect(l3[:]), ACT.Exp, bias=ea_bias[:, c], scale=tau_c[:, c])
 
-        den = [keep.tile([P, S], F32, name=f"den{t}", tag=tag, align_bytes=64) for t, tag in enumerate(("ws14_raw", "w3", "xs_three", "ws3"))]
         for t in tiles:
+            nc.vector.tensor_scalar(wide[t][:, :S], b_ps[t][:], 1.0, None, ALU.mult, ALU.max, accum_out=top[:, t : t + 1])
+            if t > 0:
+                look_up_b(t - 1)
+
+        xw_offs = pick("xw_offs", x_w, U32, l_offs, tag="ws2_raw")
+        look_up_b(PACK - 1)
+        ws14 = deal(nc.vector.tensor_copy, "ws14", ws14_raw, U8)
+        y_ps = product("y_ps", "pa", w1, ws14, 0, xw_offs[:], xs_offs[:], S)
+        y_at = rows("y_at")
+        den = rows("den")
+        num = rows("num", tag="ad")
+
+        def make_den(t):
             nc.vector.tensor_tensor(den[t][:], ad[t][:].indirect(l2[:]), ad_twin[t][:], ALU.add)
-        num = rows("diff", tag="ad")
+
+        def fetch_y(t):
+            nc.vector.tensor_copy(y[t][:, :S], y_ps[t][:])
+
+        def look_up_y(t):
+            nc.scalar.activation(y_at[t][:], y[t][:].indirect(l1[:]), ACT.Copy)
 
         def make_num(t):
             nc.vector.tensor_tensor(num[t][:], y[t][:, :S], y_at[t][:], ALU.subtract)
@@ -189,11 +184,14 @@ def tile_picked_trionormbpxbemx_none_po_kernel(
         u = rows("u")
         z = keep.tile([P, PACK, S], BF16, name="z")
 
+        def square_den(t):
+            nc.scalar.activation(den[t][:], den[t][:], ACT.Square, bias=0.5)
+
+        def invert_den(t):
+            nc.scalar.activation(wide[PACK - 1 - t][:, :S], den[t][:], ACT.Abs_reciprocal_sqrt)
+
         def make_m1(t):
-            inv = wide[PACK - 1 - t][:, :S]
-            nc.scalar.activation(inv, den[t][:], ACT.Square, bias=0.5)
-            nc.scalar.activation(inv, inv, ACT.Abs_reciprocal_sqrt)
-            nc.vector.tensor_tensor(m1[t][:, :S], num[t][:], inv, ALU.mult)
+            nc.vector.tensor_tensor(m1[t][:, :S], num[t][:], wide[PACK - 1 - t][:, :S], ALU.mult)
 
         def look_up_m1(t, j):
             nc.scalar.activation(u[t][:, j], m1[t][:].indirect(part(l4, j)), ACT.Copy)
@@ -217,8 +215,7 @@ def tile_picked_trionormbpxbemx_none_po_kernel(
         h = wide
         own = rows("own")
 
-        def make_h(hf, on_scalar, tag):
-            z_grouped = interleave(f"z_grouped{hf}", z[:, :, cols(hf)], on_scalar)
+        def make_h(hf, z_grouped, tag):
             z_codes = keep.tile([P, HALF], U32, name=f"z_codes{hf}", align_bytes=64)
             z_scales = keep.tile([P, HALF], U8, name=f"z_scales{hf}", align_bytes=64)
             nc.vector.quantize_mx(out=z_codes[:].bitcast(FP8X4), scales=z_scales[:], in_=z_grouped[:].rearrange("p j t -> p (j t)"))
@@ -228,44 +225,76 @@ def tile_picked_trionormbpxbemx_none_po_kernel(
             nc.scalar.activation(own[t][:, cols(hf)], src, ACT.Sigmoid, bias=sg_bias[:, t : t + 1], scale=sl_c[:, t : t + 1])
 
         whole = slice(0, S)
+        gn_twice = keep.tile([P, PACK], F32, name="gn_twice", tag="top")
+        gn_half = keep.tile([P, PACK], F32, name="gn_half", tag="xs_two", align_bytes=64)
+        sg_bias = keep.tile([P, PACK], F32, name="sg_bias", tag="ea_bias")
+        first, second = cols(0), cols(1)
+        make_den(0)
+        fetch_y(0)
+        fetch_y(1)
+        make_den(1)
+        fetch_y(2)
+        make_den(2)
+        look_up_y(0)
+        square_den(0)
+        look_up_y(1)
+        square_den(1)
         make_num(0)
+        fetch_y(3)
+        make_den(3)
         make_num(1)
+        invert_den(0)
+        invert_den(1)
         make_m1(0)
-        make_num(2)
         make_m1(1)
-        make_num(3)
+        nc.vector.tensor_scalar(gn_twice[:], gn_c[:], 2.0, None, ALU.mult)
+        nc.vector.scalar_tensor_tensor(sg_bias[:], sl_c[:], -1.0, th_c[:], ALU.mult, ALU.mult)
+        nc.vector.tensor_scalar(gn_half[:], gn_twice[:], -0.25, None, ALU.mult)
+        look_up_y(2)
+        make_num(2)
         look_up_m1(0, whole)
+        look_up_m1(1, whole)
         subtract_m1(0, whole)
         weigh(0, whole)
-        make_m1(2)
-        make_z(0, whole)
-        look_up_m1(1, whole)
         subtract_m1(1, whole)
+        make_z(0, whole)
         weigh(1, whole)
-        make_m1(3)
+        square_den(2)
+        look_up_y(3)
+        invert_den(2)
+        square_den(3)
+        invert_den(3)
+        make_num(3)
+        make_m1(2)
         make_z(1, whole)
-        for hf in halves:
-            for t in (2, 3):
-                look_up_m1(t, cols(hf))
-        w4 = deal(nc.scalar.copy, "w4", w4_raw, U32, tag="m10")
-        for step in (subtract_m1, weigh, make_z):
-            for t in (2, 3):
-                step(t, cols(0))
-        for step in (subtract_m1, weigh):
-            for t in (2, 3):
-                step(t, cols(1))
-        h_first = make_h(0, HALF, "pb")
+        make_m1(3)
+        for t in (2, 3):
+            for j in (first, second):
+                look_up_m1(t, j)
+        w4 = deal(nc.scalar.copy, "w4", w4_raw, U32, tag="m11")
+        subtract_m1(2, first)
+        subtract_m1(2, second)
+        weigh(2, first)
+        subtract_m1(3, first)
+        make_z(2, first)
+        weigh(3, first)
+        subtract_m1(3, second)
+        make_z(3, first)
+        weigh(2, second)
+        grouped = interleave("z_grouped0", z[:, :, first], SCALAR_SHARE)
+        weigh(3, second)
+        h_first = make_h(0, grouped, "pa")
         for t in tiles:
             make_own(0, t, h_first[t][:, :HALF])
         for t in (0, 1):
-            nc.scalar.copy(h[t][:, cols(0)], h_first[t][:, :HALF])
+            nc.scalar.copy(h[t][:, first], h_first[t][:, :HALF])
         for t in (2, 3):
-            make_z(t, cols(1))
-        h_second = make_h(1, 0, "pa")
+            make_z(t, second)
+        h_second = make_h(1, interleave("z_grouped1", z[:, :, second], 0), "pb")
         for t in (2, 3):
-            nc.vector.tensor_copy(h[t][:, cols(0)], h_first[t][:, :HALF])
+            nc.vector.tensor_copy(h[t][:, first], h_first[t][:, :HALF])
         for t in tiles:
-            (nc.scalar.copy if t == 0 else nc.vector.tensor_copy)(h[t][:, cols(1)], h_second[t][:, :HALF])
+            (nc.scalar.copy if t == 0 else nc.vector.tensor_copy)(h[t][:, second], h_second[t][:, :HALF])
 
         out_rows = out_0.rearrange("(p t) j -> p t j", t=PACK)
         out_words = out_1[0].rearrange("p n t -> p (n t)").bitcast(I32)

@@ -17,9 +17,9 @@ PACK = 4
 TOKENS = 2048
 S = 512
 HALF = S // 2
-LIST_COLS = S // 16
-SCALAR_SHARE = 96
+PER_COLUMN = 16
 SPARE = 16
+SCALAR_SHARE = 96
 FLOPS = 4 * 2 * 512 * 512 * 512
 
 
@@ -29,31 +29,29 @@ def tile_picked_trionormbpxbemx_none_po_kernel(
 ):
     nc = tc.nc
     tiles = range(PACK)
-    halves = range(2)
+    last = PACK - 1
+    whole, first, second = slice(0, S), slice(0, HALF), slice(HALF, S)
 
     with ExitStack() as ctx:
         keep = ctx.enter_context(tc.tile_pool(name="keep", bufs=1))
         psum = ctx.enter_context(tc.psum_pool(name="psum", bufs=1))
 
-        def cols(half):
-            return slice(half * HALF, (half + 1) * HALF)
-
         def load_list(name, src):
-            tile = keep.tile([P, LIST_COLS], U16, name=name)
+            tile = keep.tile([P, S // PER_COLUMN], U16, name=name)
             nc.sync.dma_start(tile[:], src)
             return tile
 
-        def part(lst, j):
-            return lst[:, j.start // 16 : j.stop // 16]
+        def entries(lst, j):
+            return lst[:, j.start // PER_COLUMN : j.stop // PER_COLUMN]
 
         def load_words(name, src, width):
-            tile = keep.tile([P, width], U32, name=name, tag=name, align_bytes=64)
+            tile = keep.tile([P, width], U32, name=name, align_bytes=64)
             nc.sync.dma_start(tile[:].bitcast(I32), src[0].rearrange("p n t -> p (n t)").bitcast(I32))
             return tile
 
         def scale_tile(name, width):
             tile = keep.tile([P, width], U8, name=name, tag=name, align_bytes=64)
-            nc.vector.memset(tile[:].bitcast(I32), 0)
+            nc.gpsimd.memset(tile[:].bitcast(I32), 0)
             return tile
 
         def load_scale_rows(tile, src, row):
@@ -65,28 +63,29 @@ def tile_picked_trionormbpxbemx_none_po_kernel(
             nc.sync.dma_start(tile[:], src.rearrange("(p t) o -> p (t o)", t=PACK))
             return tile
 
-        def deal(engine_copy, name, raw, dtype, tag=None):
-            tile = keep.tile([P, PACK, P], dtype, name=name, tag=tag or name, align_bytes=64)
-            engine_copy(tile[:].rearrange("p t m -> p m t"), raw[:].rearrange("p (m t) -> p m t", t=PACK))
+        def deal(copy, name, raw, dtype):
+            tile = keep.tile([P, PACK, P], dtype, name=name, align_bytes=64)
+            copy(tile[:].rearrange("p t m -> p m t"), raw[:].rearrange("p (m t) -> p m t", t=PACK))
             return tile
 
-        def rows(name, dtype=F32, tag=None):
-            return [keep.tile([P, S], dtype, name=f"{name}{t}", tag=f"{tag or name}{t}", align_bytes=64) for t in tiles]
+        def rows(name, tag=None):
+            return [keep.tile([P, S], F32, name=f"{name}{t}", tag=f"{tag or name}{t}", align_bytes=64) for t in tiles]
 
-        def windows(name, spare):
-            made = [keep.tile([P, S + spare], F32, name=f"{name}{t}", tag=f"{name}{t}", align_bytes=64) for t in tiles]
-            for tile in made:
-                nc.vector.memset(tile[:, S:], 0.0)
-            return made
+        def window(name):
+            tile = keep.tile([P, S + SPARE], F32, name=name, tag=name, align_bytes=64)
+            nc.scalar.copy(tile[:, S:], wide[0][:, S : S + SPARE])
+            return tile
 
         x_sc = scale_tile("x_sc", TOKENS)
         ws2_raw = scale_tile("ws2_raw", S)
         ws3_raw = scale_tile("ws3_raw", S)
         ws14_raw = scale_tile("ws14_raw", S)
-        ad = windows("ad", SPARE)
-        wide = windows("wide", S)
-        y = windows("y", SPARE)
-        m1 = windows("m1", SPARE)
+        wide = [keep.tile([P, 2 * S], F32, name=f"wide{t}") for t in tiles]
+        for tile in wide:
+            nc.gpsimd.memset(tile[:, S:], 0.0)
+        ad = [window(f"ad{t}") for t in tiles]
+        y = [window(f"y{t}") for t in tiles]
+        m1 = [window(f"m1{t}") for t in (0, 1)] + [keep.tile([P, S], F32, name=f"m1{t}") for t in (2, 3)]
 
         l_two = load_list("l_two", two)
         l_three = load_list("l_three", three)
@@ -100,6 +99,8 @@ def tile_picked_trionormbpxbemx_none_po_kernel(
         tau_c = load_column("tau_c", tau)
         l3 = load_list("l3", n3)
         w1_raw = load_words("w1_raw", w1_words, S)
+        w4_raw = load_words("w4_raw", w4_words, S)
+        gn_c = load_column("gn_c", gn)
         load_scale_rows(ws14_raw, w1_scales, 0)
         load_scale_rows(ws14_raw, w4_scales, 4)
         l2 = load_list("l2", n2)
@@ -110,10 +111,10 @@ def tile_picked_trionormbpxbemx_none_po_kernel(
             nc.vector.tensor_copy(tile[:], table[:].indirect(lst[:]))
             return tile
 
-        def product(name, tag, w, w_sc, row, codes, scales, width):
+        def product(name, bank_set, w, w_sc, row, codes, scales, width):
             banks = []
             for t in tiles:
-                bank = psum.tile([P, S], F32, name=f"{name}{t}", tag=f"{tag}{t}")
+                bank = psum.tile([P, S], F32, name=f"{name}{t}", tag=f"{bank_set}{t}")
                 nc.tensor.matmul_mx(
                     out=bank[:, :width], lhsT=w[:, t, :].bitcast(FP8X4), lhsT_scale=w_sc[row:P, t, :],
                     rhs=codes.bitcast(FP8X4), rhs_scale=scales, start=True, stop=True,
@@ -133,10 +134,13 @@ def tile_picked_trionormbpxbemx_none_po_kernel(
             nc.scalar.activation(ad[t][:, :S], d_ps[t][:], ACT.Abs)
             nc.sync.dma_start(ad_twin[t][:], ad[t][:, :S])
         w1 = deal(nc.scalar.copy, "w1", w1_raw, U32)
+        w4 = deal(nc.scalar.copy, "w4", w4_raw, U32)
+        gn_twice = keep.tile([P, PACK], F32, name="gn_twice")
+        nc.scalar.activation(gn_twice[:], gn_c[:], ACT.Copy, scale=2.0)
+        gn_minus_half = keep.tile([P, PACK], F32, name="gn_minus_half")
+        nc.scalar.activation(gn_minus_half[:], gn_c[:], ACT.Copy, scale=-0.5)
 
-        gn_c = load_column("gn_c", gn)
         l4 = load_list("l4", n4)
-        w4_raw = load_words("w4_raw", w4_words, S)
         sl_c = load_column("sl_c", sl)
         th_c = load_column("th_c", th)
         l5 = load_list("l5", n5)
@@ -148,10 +152,10 @@ def tile_picked_trionormbpxbemx_none_po_kernel(
         b_ps = product("b_ps", "pb", w3, ws3, 0, xw_three[:], xs_three[:], S)
         xs_offs = pick("xs_offs", x_sc, U8, l_offs, tag="ws3_raw")
         ea = rows("ea")
-        top = keep.tile([P, PACK], F32, name="top", tag="top")
-        ea_bias = keep.tile([P, PACK], F32, name="ea_bias", tag="ea_bias")
+        top = keep.tile([P, PACK], F32, name="top")
+        ea_bias = keep.tile([P, PACK], F32, name="ea_bias", tag="bias")
 
-        def look_up_b(t):
+        def make_ea(t):
             c = slice(t, t + 1)
             nc.vector.tensor_scalar(ea_bias[:, c], top[:, c], tau_c[:, c], -1.0, ALU.mult, ALU.mult)
             nc.scalar.activation(ea[t][:], wide[t][:].indirect(l3[:]), ACT.Exp, bias=ea_bias[:, c], scale=tau_c[:, c])
@@ -159,15 +163,19 @@ def tile_picked_trionormbpxbemx_none_po_kernel(
         for t in tiles:
             nc.vector.tensor_scalar(wide[t][:, :S], b_ps[t][:], 1.0, None, ALU.mult, ALU.max, accum_out=top[:, t : t + 1])
             if t > 0:
-                look_up_b(t - 1)
-
+                make_ea(t - 1)
         xw_offs = pick("xw_offs", x_w, U32, l_offs, tag="ws2_raw")
-        look_up_b(PACK - 1)
+        make_ea(last)
+
         ws14 = deal(nc.vector.tensor_copy, "ws14", ws14_raw, U8)
         y_ps = product("y_ps", "pa", w1, ws14, 0, xw_offs[:], xs_offs[:], S)
         y_at = rows("y_at")
         den = rows("den")
         num = rows("num", tag="ad")
+        u = rows("u")
+        z = keep.tile([P, PACK, S], BF16, name="z")
+        sg_bias = keep.tile([P, PACK], F32, name="sg_bias", tag="bias")
+        inverse = [wide[last - t][:, :S] for t in tiles]
 
         def make_den(t):
             nc.vector.tensor_tensor(den[t][:], ad[t][:].indirect(l2[:]), ad_twin[t][:], ALU.add)
@@ -178,23 +186,20 @@ def tile_picked_trionormbpxbemx_none_po_kernel(
         def look_up_y(t):
             nc.scalar.activation(y_at[t][:], y[t][:].indirect(l1[:]), ACT.Copy)
 
-        def make_num(t):
-            nc.vector.tensor_tensor(num[t][:], y[t][:, :S], y_at[t][:], ALU.subtract)
-
-        u = rows("u")
-        z = keep.tile([P, PACK, S], BF16, name="z")
-
         def square_den(t):
             nc.scalar.activation(den[t][:], den[t][:], ACT.Square, bias=0.5)
 
-        def invert_den(t):
-            nc.scalar.activation(wide[PACK - 1 - t][:, :S], den[t][:], ACT.Abs_reciprocal_sqrt)
+        def invert_den(t, lacking):
+            nc.scalar.activation(inverse[t], den[t][:], ACT.Abs_reciprocal_sqrt, bias=lacking)
+
+        def make_num(t):
+            nc.vector.tensor_tensor(num[t][:], y[t][:, :S], y_at[t][:], ALU.subtract)
 
         def make_m1(t):
-            nc.vector.tensor_tensor(m1[t][:, :S], num[t][:], wide[PACK - 1 - t][:, :S], ALU.mult)
+            nc.vector.tensor_tensor(m1[t][:, :S], num[t][:], inverse[t], ALU.mult)
 
         def look_up_m1(t, j):
-            nc.scalar.activation(u[t][:, j], m1[t][:].indirect(part(l4, j)), ACT.Copy)
+            nc.scalar.activation(u[t][:, j], m1[t][:].indirect(entries(l4, j)), ACT.Copy)
 
         def subtract_m1(t, j):
             nc.vector.tensor_tensor(u[t][:, j], m1[t][:, j], u[t][:, j], ALU.subtract)
@@ -203,75 +208,63 @@ def tile_picked_trionormbpxbemx_none_po_kernel(
             nc.vector.scalar_tensor_tensor(u[t][:, j], u[t][:, j], gn_twice[:, t : t + 1], ea[t][:, j], ALU.mult, ALU.mult)
 
         def make_z(t, j):
-            nc.vector.scalar_tensor_tensor(z[:, t, j], b_ps[t][:, j], gn_half[:, t : t + 1], u[t][:, j], ALU.mult, ALU.add)
+            nc.vector.scalar_tensor_tensor(z[:, t, j], b_ps[t][:, j], gn_minus_half[:, t : t + 1], u[t][:, j], ALU.mult, ALU.add)
 
-        def interleave(name, src, on_scalar):
+        def regroup(name, src, on_scalar):
             tile = keep.tile([P, HALF, PACK], BF16, name=name, align_bytes=64)
             for copy, a, e in ((nc.scalar.copy, 0, on_scalar), (nc.vector.tensor_copy, on_scalar, HALF)):
                 if e > a:
                     copy(tile[:, a:e, :].rearrange("p (c i) t -> p c t i", i=4), src[:, :, a:e].rearrange("p t (c i) -> p c t i", i=4))
             return tile
 
-        h = wide
-        own = rows("own")
-
-        def make_h(hf, z_grouped, tag):
-            z_codes = keep.tile([P, HALF], U32, name=f"z_codes{hf}", align_bytes=64)
-            z_scales = keep.tile([P, HALF], U8, name=f"z_scales{hf}", align_bytes=64)
-            nc.vector.quantize_mx(out=z_codes[:].bitcast(FP8X4), scales=z_scales[:], in_=z_grouped[:].rearrange("p j t -> p (j t)"))
-            return product(f"h_ps{hf}", tag, w4, ws14, 4, z_codes[:], z_scales[:], HALF)
-
-        def make_own(hf, t, src):
-            nc.scalar.activation(own[t][:, cols(hf)], src, ACT.Sigmoid, bias=sg_bias[:, t : t + 1], scale=sl_c[:, t : t + 1])
-
-        whole = slice(0, S)
-        gn_twice = keep.tile([P, PACK], F32, name="gn_twice", tag="top")
-        gn_half = keep.tile([P, PACK], F32, name="gn_half", tag="xs_two", align_bytes=64)
-        sg_bias = keep.tile([P, PACK], F32, name="sg_bias", tag="ea_bias")
-        first, second = cols(0), cols(1)
         make_den(0)
         fetch_y(0)
         fetch_y(1)
         make_den(1)
         fetch_y(2)
-        make_den(2)
         look_up_y(0)
         square_den(0)
-        look_up_y(1)
-        square_den(1)
+        invert_den(0, 0.0)
         make_num(0)
+        make_den(2)
         fetch_y(3)
-        make_den(3)
-        make_num(1)
-        invert_den(0)
-        invert_den(1)
         make_m1(0)
-        make_m1(1)
-        nc.vector.tensor_scalar(gn_twice[:], gn_c[:], 2.0, None, ALU.mult)
-        nc.vector.scalar_tensor_tensor(sg_bias[:], sl_c[:], -1.0, th_c[:], ALU.mult, ALU.mult)
-        nc.vector.tensor_scalar(gn_half[:], gn_twice[:], -0.25, None, ALU.mult)
-        look_up_y(2)
-        make_num(2)
-        look_up_m1(0, whole)
-        look_up_m1(1, whole)
-        subtract_m1(0, whole)
-        weigh(0, whole)
-        subtract_m1(1, whole)
-        make_z(0, whole)
-        weigh(1, whole)
-        square_den(2)
-        look_up_y(3)
-        invert_den(2)
-        square_den(3)
-        invert_den(3)
-        make_num(3)
-        make_m1(2)
-        make_z(1, whole)
-        make_m1(3)
+        make_den(3)
+        for t in range(1, PACK):
+            look_up_y(t)
+            if t < last:
+                square_den(t)
+                look_up_m1(t - 1, whole)
+                invert_den(t, 0.0)
+            make_num(t)
+            if t > 1:
+                make_z(t - 2, whole)
+            if t == last - 1:
+                nc.vector.scalar_tensor_tensor(den[last][:], den[last][:], 1.0, den[last][:], ALU.add, ALU.mult)
+                nc.vector.scalar_tensor_tensor(sg_bias[:], sl_c[:], -1.0, th_c[:], ALU.mult, ALU.mult)
+            if t < last:
+                subtract_m1(t - 1, whole)
+                make_m1(t)
+                weigh(t - 1, whole)
+            else:
+                invert_den(t, 0.25)
+                make_m1(t)
+
+        h = wide
+        own = rows("own")
+
+        def make_h(name, z_grouped, bank_set):
+            z_codes = keep.tile([P, HALF], U32, name=f"z_codes_{name}", align_bytes=64)
+            z_scales = keep.tile([P, HALF], U8, name=f"z_scales_{name}", align_bytes=64)
+            nc.vector.quantize_mx(out=z_codes[:].bitcast(FP8X4), scales=z_scales[:], in_=z_grouped[:].rearrange("p j t -> p (j t)"))
+            return product(f"h_ps_{name}", bank_set, w4, ws14, 4, z_codes[:], z_scales[:], HALF)
+
+        def make_own(t, j, src):
+            nc.scalar.activation(own[t][:, j], src, ACT.Sigmoid, bias=sg_bias[:, t : t + 1], scale=sl_c[:, t : t + 1])
+
         for t in (2, 3):
             for j in (first, second):
                 look_up_m1(t, j)
-        w4 = deal(nc.scalar.copy, "w4", w4_raw, U32, tag="m11")
         subtract_m1(2, first)
         subtract_m1(2, second)
         weigh(2, first)
@@ -280,55 +273,57 @@ def tile_picked_trionormbpxbemx_none_po_kernel(
         weigh(3, first)
         subtract_m1(3, second)
         make_z(3, first)
+        z_first = regroup("z_first", z[:, :, first], 0)
         weigh(2, second)
-        grouped = interleave("z_grouped0", z[:, :, first], SCALAR_SHARE)
-        weigh(3, second)
-        h_first = make_h(0, grouped, "pa")
+        h_first = make_h("first", z_first, "pa")
         for t in tiles:
-            make_own(0, t, h_first[t][:, :HALF])
+            make_own(t, first, h_first[t][:, :HALF])
         for t in (0, 1):
             nc.scalar.copy(h[t][:, first], h_first[t][:, :HALF])
+        weigh(3, second)
         for t in (2, 3):
             make_z(t, second)
-        h_second = make_h(1, interleave("z_grouped1", z[:, :, second], 0), "pb")
+        h_second = make_h("second", regroup("z_second", z[:, :, second], 0), "pb")
         for t in (2, 3):
             nc.vector.tensor_copy(h[t][:, first], h_first[t][:, :HALF])
-        for t in tiles:
-            (nc.scalar.copy if t == 0 else nc.vector.tensor_copy)(h[t][:, second], h_second[t][:, :HALF])
+        early = 1
+        nc.vector.tensor_copy(h[0][:, second], h_second[0][:, :HALF])
+        make_own(early, second, h_second[early][:, :HALF])
+        for t in (2, 3, early):
+            nc.vector.tensor_copy(h[t][:, second], h_second[t][:, :HALF])
 
         out_rows = out_0.rearrange("(p t) j -> p t j", t=PACK)
         out_words = out_1[0].rearrange("p n t -> p (n t)").bitcast(I32)
-        o_scales = keep.tile([P, S], U8, name="o_scales", align_bytes=64)
+        out_scales = keep.tile([P, S], U8, name="out_scales", align_bytes=64)
         sg = rows("sg")
-        h7 = rows("h7")
+        h_at = rows("h_at")
         res = keep.tile([P, PACK, S], F32, name="res")
 
         def finish(t, j):
             nc.vector.tensor_tensor(res[:, t, j], res[:, t, j], sg[t][:, j], ALU.add)
             nc.sync.dma_start(out_rows[:, t, j], res[:, t, j])
 
-        def hand_on(hf, grouped):
-            o_codes = keep.tile([P, HALF], U32, name=f"o_codes{hf}", align_bytes=64)
-            nc.vector.quantize_mx(out=o_codes[:].bitcast(FP8X4), scales=o_scales[:, cols(hf)], in_=grouped[:].rearrange("p j t -> p (j t)"))
-            nc.sync.dma_start(out_words[:, cols(hf)], o_codes[:].bitcast(I32))
+        def hand_on(name, j, grouped):
+            codes = keep.tile([P, HALF], U32, name=name, align_bytes=64)
+            nc.vector.quantize_mx(out=codes[:].bitcast(FP8X4), scales=out_scales[:, j], in_=grouped[:].rearrange("p j t -> p (j t)"))
+            nc.sync.dma_start(out_words[:, j], codes[:].bitcast(I32))
 
-        last = PACK - 1
-        steps = [(t, whole) for t in range(last)] + [(last, cols(hf)) for hf in halves]
+        steps = [(t, whole) for t in range(last)] + [(last, first), (last, second)]
         for i, (t, j) in enumerate(steps):
             c = slice(t, t + 1)
-            if j != cols(1):
-                make_own(1, t, h[t][:, cols(1)])
-            nc.scalar.activation(sg[t][:, j], h[t][:].indirect(part(l5, j)), ACT.Sigmoid, bias=sg_bias[:, c], scale=sl_c[:, c])
-            nc.scalar.activation(h7[t][:, j], h[t][:].indirect(part(l7, j)), ACT.Copy)
-            nc.vector.tensor_tensor(res[:, t, j], h[t][:].indirect(part(l6, j)), own[t][:, j], ALU.mult)
+            if j != second and t != early:
+                make_own(t, second, h[t][:, second])
+            nc.scalar.activation(sg[t][:, j], h[t][:].indirect(entries(l5, j)), ACT.Sigmoid, bias=sg_bias[:, c], scale=sl_c[:, c])
+            nc.scalar.activation(h_at[t][:, j], h[t][:].indirect(entries(l7, j)), ACT.Copy)
+            nc.vector.tensor_tensor(res[:, t, j], h[t][:].indirect(entries(l6, j)), own[t][:, j], ALU.mult)
             if i > 0:
                 finish(*steps[i - 1])
-            if j == cols(1):
-                grouped = interleave("o_grouped0", res[:, :, cols(0)], 0)
-            nc.vector.tensor_tensor(sg[t][:, j], sg[t][:, j], h7[t][:, j], ALU.mult)
-        hand_on(0, grouped)
+            if j == second:
+                res_first = regroup("res_first", res[:, :, first], 0)
+            nc.vector.tensor_tensor(sg[t][:, j], sg[t][:, j], h_at[t][:, j], ALU.mult)
+        hand_on("codes_first", first, res_first)
         finish(*steps[-1])
-        hand_on(1, interleave("o_grouped1", res[:, :, cols(1)], SCALAR_SHARE))
+        hand_on("codes_second", second, regroup("res_second", res[:, :, second], SCALAR_SHARE))
         for q in range(4):
             queue = nc.sync if q % 2 else nc.scalar
-            queue.dma_start(out_2[0, 4 * q : 4 * q + 4, :].bitcast(I32), o_scales[32 * q : 32 * q + 4, :].bitcast(I32))
+            queue.dma_start(out_2[0, 4 * q : 4 * q + 4, :].bitcast(I32), out_scales[32 * q : 32 * q + 4, :].bitcast(I32))

from contextlib import ExitStack

import concourse.mybir as mybir

F32 = mybir.dt.float32
BF16 = mybir.dt.bfloat16
I32 = mybir.dt.int32
U32 = mybir.dt.uint32
U16 = mybir.dt.uint16
U8 = mybir.dt.uint8
FP8X4 = mybir.dt.float8_e4m3fn_x4
ALU = mybir.AluOpType
ACT = mybir.ActivationFunctionType

P = 128
PACK = 4
TOKENS = 2048
S = 512
HALF = S // 2
PER_COLUMN = 16
SPARE = 16
SCALAR_SHARE = 96
FLOPS = 4 * 2 * 512 * 512 * 512


def tile_picked_trionormbpxbemx_none_po_kernel(
    tc, x_words, x_scales, w1_words, w1_scales, w2_words, w2_scales, w3_words, w3_scales, tau, gn,
    w4_words, w4_scales, sl, th, offs, two, three, n1, n2, n3, n4, n5, n6, n7, out_0, out_1, out_2,
):
    nc = tc.nc
    tiles = range(PACK)
    last = PACK - 1
    whole, first, second = slice(0, S), slice(0, HALF), slice(HALF, S)

    with ExitStack() as ctx:
        keep = ctx.enter_context(tc.tile_pool(name="keep", bufs=1))
        psum = ctx.enter_context(tc.psum_pool(name="psum", bufs=1))

        def load_list(name, src):
            tile = keep.tile([P, S // PER_COLUMN], U16, name=name)
            nc.sync.dma_start(tile[:], src)
            return tile

        def entries(lst, j):
            return lst[:, j.start // PER_COLUMN : j.stop // PER_COLUMN]

        def load_words(name, src, width):
            tile = keep.tile([P, width], U32, name=name, align_bytes=64)
            nc.sync.dma_start(tile[:].bitcast(I32), src[0].rearrange("p n t -> p (n t)").bitcast(I32))
            return tile

        def scale_tile(name, width):
            tile = keep.tile([P, width], U8, name=name, tag=name, align_bytes=64)
            nc.gpsimd.memset(tile[:].bitcast(I32), 0)
            return tile

        def load_scale_rows(tile, src, row):
            for q in range(4):
                nc.sync.dma_start(tile[32 * q + row : 32 * q + row + 4, :].bitcast(I32), src[0, 4 * q : 4 * q + 4, :].bitcast(I32))

        def load_column(name, src):
            tile = keep.tile([P, PACK], F32, name=name)
            nc.sync.dma_start(tile[:], src.rearrange("(p t) o -> p (t o)", t=PACK))
            return tile

        def deal(copy, name, raw, dtype):
            tile = keep.tile([P, PACK, P], dtype, name=name, align_bytes=64)
            copy(tile[:].rearrange("p t m -> p m t"), raw[:].rearrange("p (m t) -> p m t", t=PACK))
            return tile

        def rows(name, tag=None):
            return [keep.tile([P, S], F32, name=f"{name}{t}", tag=f"{tag or name}{t}", align_bytes=64) for t in tiles]

        def window(name):
            tile = keep.tile([P, S + SPARE], F32, name=name, tag=name, align_bytes=64)
            nc.scalar.copy(tile[:, S:], wide[0][:, S : S + SPARE])
            return tile

        x_sc = scale_tile("x_sc", TOKENS)
        ws2_raw = scale_tile("ws2_raw", S)
        ws3_raw = scale_tile("ws3_raw", S)
        ws14_raw = scale_tile("ws14_raw", S)
        wide = [keep.tile([P, 2 * S], F32, name=f"wide{t}") for t in tiles]
        for tile in wide:
            nc.gpsimd.memset(tile[:, S:], 0.0)
        ad = [window(f"ad{t}") for t in tiles]
        y = [window(f"y{t}") for t in tiles]
        m1 = [window(f"m1{t}") for t in (0, 1)] + [keep.tile([P, S], F32, name=f"m1{t}") for t in (2, 3)]

        l_two = load_list("l_two", two)
        l_three = load_list("l_three", three)
        load_scale_rows(x_sc, x_scales, 0)
        x_w = load_words("x_w", x_words, TOKENS)
        w2_raw = load_words("w2_raw", w2_words, S)
        load_scale_rows(ws2_raw, w2_scales, 0)
        l_offs = load_list("l_offs", offs)
        w3_raw = load_words("w3_raw", w3_words, S)
        load_scale_rows(ws3_raw, w3_scales, 0)
        tau_c = load_column("tau_c", tau)
        l3 = load_list("l3", n3)
        w1_raw = load_words("w1_raw", w1_words, S)
        w4_raw = load_words("w4_raw", w4_words, S)
        gn_c = load_column("gn_c", gn)
        load_scale_rows(ws14_raw, w1_scales, 0)
        load_scale_rows(ws14_raw, w4_scales, 4)
        l2 = load_list("l2", n2)
        l1 = load_list("l1", n1)

        def pick(name, table, dtype, lst, tag=None):
            tile = keep.tile([P, S], dtype, name=name, tag=tag or name, align_bytes=64)
            nc.vector.tensor_copy(tile[:], table[:].indirect(lst[:]))
            return tile

        def product(name, bank_set, w, w_sc, row, codes, scales, width):
            banks = []
            for t in tiles:
                bank = psum.tile([P, S], F32, name=f"{name}{t}", tag=f"{bank_set}{t}")
                nc.tensor.matmul_mx(
                    out=bank[:, :width], lhsT=w[:, t, :].bitcast(FP8X4), lhsT_scale=w_sc[row:P, t, :],
                    rhs=codes.bitcast(FP8X4), rhs_scale=scales, start=True, stop=True,
                )
                banks.append(bank)
            return banks

        xs_two = pick("xs_two", x_sc, U8, l_two)
        xs_three = pick("xs_three", x_sc, U8, l_three)
        w2 = deal(nc.scalar.copy, "w2", w2_raw, U32)
        ws2 = deal(nc.vector.tensor_copy, "ws2", ws2_raw, U8)
        xw_two = pick("xw_two", x_w, U32, l_two)
        w3 = deal(nc.scalar.copy, "w3", w3_raw, U32)
        d_ps = product("d_ps", "pa", w2, ws2, 0, xw_two[:], xs_two[:], S)
        ad_twin = rows("ad_twin")
        for t in tiles:
            nc.scalar.activation(ad[t][:, :S], d_ps[t][:], ACT.Abs)
            nc.sync.dma_start(ad_twin[t][:], ad[t][:, :S])
        w1 = deal(nc.scalar.copy, "w1", w1_raw, U32)
        w4 = deal(nc.scalar.copy, "w4", w4_raw, U32)
        gn_twice = keep.tile([P, PACK], F32, name="gn_twice")
        nc.scalar.activation(gn_twice[:], gn_c[:], ACT.Copy, scale=2.0)
        gn_minus_half = keep.tile([P, PACK], F32, name="gn_minus_half")
        nc.scalar.activation(gn_minus_half[:], gn_c[:], ACT.Copy, scale=-0.5)

        l4 = load_list("l4", n4)
        sl_c = load_column("sl_c", sl)
        th_c = load_column("th_c", th)
        l5 = load_list("l5", n5)
        l6 = load_list("l6", n6)
        l7 = load_list("l7", n7)

        xw_three = pick("xw_three", x_w, U32, l_three, tag="ws2_raw")
        ws3 = deal(nc.vector.tensor_copy, "ws3", ws3_raw, U8)
        b_ps = product("b_ps", "pb", w3, ws3, 0, xw_three[:], xs_three[:], S)
        xs_offs = pick("xs_offs", x_sc, U8, l_offs, tag="ws3_raw")
        ea = rows("ea")
        top = keep.tile([P, PACK], F32, name="top")
        ea_bias = keep.tile([P, PACK], F32, name="ea_bias", tag="bias")

        def make_ea(t):
            c = slice(t, t + 1)
            nc.vector.tensor_scalar(ea_bias[:, c], top[:, c], tau_c[:, c], -1.0, ALU.mult, ALU.mult)
            nc.scalar.activation(ea[t][:], wide[t][:].indirect(l3[:]), ACT.Exp, bias=ea_bias[:, c], scale=tau_c[:, c])

        for t in tiles:
            nc.vector.tensor_scalar(wide[t][:, :S], b_ps[t][:], 1.0, None, ALU.mult, ALU.max, accum_out=top[:, t : t + 1])
            if t > 0:
                make_ea(t - 1)
        xw_offs = pick("xw_offs", x_w, U32, l_offs, tag="ws2_raw")
        make_ea(last)

        ws14 = deal(nc.vector.tensor_copy, "ws14", ws14_raw, U8)
        y_ps = product("y_ps", "pa", w1, ws14, 0, xw_offs[:], xs_offs[:], S)
        y_at = rows("y_at")
        den = rows("den")
        num = rows("num", tag="ad")
        u = rows("u")
        z = keep.tile([P, PACK, S], BF16, name="z")
        sg_bias = keep.tile([P, PACK], F32, name="sg_bias", tag="bias")
        inverse = [wide[last - t][:, :S] for t in tiles]

        def make_den(t):
            nc.vector.tensor_tensor(den[t][:], ad[t][:].indirect(l2[:]), ad_twin[t][:], ALU.add)

        def fetch_y(t):
            nc.vector.tensor_copy(y[t][:, :S], y_ps[t][:])

        def look_up_y(t):
            nc.scalar.activation(y_at[t][:], y[t][:].indirect(l1[:]), ACT.Copy)

        def square_den(t):
            nc.scalar.activation(den[t][:], den[t][:], ACT.Square, bias=0.5)

        def invert_den(t, lacking):
            nc.scalar.activation(inverse[t], den[t][:], ACT.Abs_reciprocal_sqrt, bias=lacking)

        def make_num(t):
            nc.vector.tensor_tensor(num[t][:], y[t][:, :S], y_at[t][:], ALU.subtract)

        def make_m1(t):
            nc.vector.tensor_tensor(m1[t][:, :S], num[t][:], inverse[t], ALU.mult)

        def look_up_m1(t, j):
            nc.scalar.activation(u[t][:, j], m1[t][:].indirect(entries(l4, j)), ACT.Copy)

        def subtract_m1(t, j):
            nc.vector.tensor_tensor(u[t][:, j], m1[t][:, j], u[t][:, j], ALU.subtract)

        def weigh(t, j):
            nc.vector.scalar_tensor_tensor(u[t][:, j], u[t][:, j], gn_twice[:, t : t + 1], ea[t][:, j], ALU.mult, ALU.mult)

        def make_z(t, j):
            nc.vector.scalar_tensor_tensor(z[:, t, j], b_ps[t][:, j], gn_minus_half[:, t : t + 1], u[t][:, j], ALU.mult, ALU.add)

        def regroup(name, src, on_scalar):
            tile = keep.tile([P, HALF, PACK], BF16, name=name, align_bytes=64)
            for copy, a, e in ((nc.scalar.copy, 0, on_scalar), (nc.vector.tensor_copy, on_scalar, HALF)):
                if e > a:
                    copy(tile[:, a:e, :].rearrange("p (c i) t -> p c t i", i=4), src[:, :, a:e].rearrange("p t (c i) -> p c t i", i=4))
            return tile

        make_den(0)
        fetch_y(0)
        fetch_y(1)
        make_den(1)
        fetch_y(2)
        look_up_y(0)
        square_den(0)
        invert_den(0, 0.0)
        make_num(0)
        make_den(2)
        fetch_y(3)
        make_m1(0)
        make_den(3)
        for t in range(1, PACK):
            look_up_y(t)
            if t < last:
                square_den(t)
                look_up_m1(t - 1, whole)
                invert_den(t, 0.0)
            make_num(t)
            if t > 1:
                make_z(t - 2, whole)
            if t == last - 1:
                nc.vector.scalar_tensor_tensor(den[last][:], den[last][:], 1.0, den[last][:], ALU.add, ALU.mult)
                nc.vector.scalar_tensor_tensor(sg_bias[:], sl_c[:], -1.0, th_c[:], ALU.mult, ALU.mult)
            if t < last:
                subtract_m1(t - 1, whole)
                make_m1(t)
                weigh(t - 1, whole)
            else:
                invert_den(t, 0.25)
                make_m1(t)

        h = wide
        own = rows("own")

        def make_h(name, z_grouped, bank_set):
            z_codes = keep.tile([P, HALF], U32, name=f"z_codes_{name}", align_bytes=64)
            z_scales = keep.tile([P, HALF], U8, name=f"z_scales_{name}", align_bytes=64)
            nc.vector.quantize_mx(out=z_codes[:].bitcast(FP8X4), scales=z_scales[:], in_=z_grouped[:].rearrange("p j t -> p (j t)"))
            return product(f"h_ps_{name}", bank_set, w4, ws14, 4, z_codes[:], z_scales[:], HALF)

        def make_own(t, j, src):
            nc.scalar.activation(own[t][:, j], src, ACT.Sigmoid, bias=sg_bias[:, t : t + 1], scale=sl_c[:, t : t + 1])

        for t in (2, 3):
            for j in (first, second):
                look_up_m1(t, j)
        subtract_m1(2, first)
        subtract_m1(2, second)
        weigh(2, first)
        subtract_m1(3, first)
        make_z(2, first)
        weigh(3, first)
        subtract_m1(3, second)
        make_z(3, first)
        z_first = regroup("z_first", z[:, :, first], 0)
        weigh(2, second)
        h_first = make_h("first", z_first, "pa")
        for t in tiles:
            make_own(t, first, h_first[t][:, :HALF])
        for t in (0, 1):
            nc.scalar.copy(h[t][:, first], h_first[t][:, :HALF])
        weigh(3, second)
        for t in (2, 3):
            make_z(t, second)
        h_second = make_h("second", regroup("z_second", z[:, :, second], 0), "pb")
        for t in (2, 3):
            nc.vector.tensor_copy(h[t][:, first], h_first[t][:, :HALF])
        early = 1
        nc.vector.tensor_copy(h[0][:, second], h_second[0][:, :HALF])
        make_own(early, second, h_second[early][:, :HALF])
        for t in (2, 3, early):
            nc.vector.tensor_copy(h[t][:, second], h_second[t][:, :HALF])

        out_rows = out_0.rearrange("(p t) j -> p t j", t=PACK)
        out_words = out_1[0].rearrange("p n t -> p (n t)").bitcast(I32)
        out_scales = keep.tile([P, S], U8, name="out_scales", align_bytes=64)
        sg = rows("sg")
        h_at = rows("h_at")
        res = keep.tile([P, PACK, S], F32, name="res")

        def finish(t, j):
            nc.vector.tensor_tensor(res[:, t, j], res[:, t, j], sg[t][:, j], ALU.add)
            nc.sync.dma_start(out_rows[:, t, j], res[:, t, j])

        def hand_on(name, j, grouped):
            codes = keep.tile([P, HALF], U32, name=name, align_bytes=64)
            nc.vector.quantize_mx(out=codes[:].bitcast(FP8X4), scales=out_scales[:, j], in_=grouped[:].rearrange("p j t -> p (j t)"))
            nc.sync.dma_start(out_words[:, j], codes[:].bitcast(I32))

        steps = [(t, whole) for t in range(last)] + [(last, first), (last, second)]
        for i, (t, j) in enumerate(steps):
            c = slice(t, t + 1)
            if j != second and t != early:
                make_own(t, second, h[t][:, second])
            nc.scalar.activation(sg[t][:, j], h[t][:].indirect(entries(l5, j)), ACT.Sigmoid, bias=sg_bias[:, c], scale=sl_c[:, c])
            nc.scalar.activation(h_at[t][:, j], h[t][:].indirect(entries(l7, j)), ACT.Copy)
            nc.vector.tensor_tensor(res[:, t, j], h[t][:].indirect(entries(l6, j)), own[t][:, j], ALU.mult)
            if i > 0:
                finish(*steps[i - 1])
            if j == second:
                res_first = regroup("res_first", res[:, :, first], 0)
            nc.vector.tensor_tensor(sg[t][:, j], sg[t][:, j], h_at[t][:, j], ALU.mult)
        hand_on("codes_first", first, res_first)
        finish(*steps[-1])
        hand_on("codes_second", second, regroup("res_second", res[:, :, second], SCALAR_SHARE))
        for q in range(4):
            queue = nc.sync if q % 2 else nc.scalar
            queue.dma_start(out_2[0, 4 * q : 4 * q + 4, :].bitcast(I32), out_scales[32 * q : 32 * q + 4, :].bitcast(I32))
